import numpy as np
import ml_dtypes


def mxq(x, axis, fmt="e4m3"):
    dtype, down = {"e4m3": (ml_dtypes.float8_e4m3fn, 7), "e5m2": (ml_dtypes.float8_e5m2, 14)}[fmt]
    v = np.moveaxis(np.asarray(x, np.float32).astype(ml_dtypes.bfloat16).astype(np.float64), axis, -1)
    blocks = v.reshape(v.shape[:-1] + (-1, 32))
    amax = np.abs(blocks).max(-1, keepdims=True)
    byte = np.maximum(np.where(amax > 0, np.frexp(amax)[1] - 1 + 127, 0) - down, 1)
    scale = np.exp2(byte - 127.0)
    codes = (blocks / scale).astype(np.float32).astype(dtype).astype(np.float64)
    return np.moveaxis((codes * scale).reshape(v.shape), -1, axis)


WIDE = False


def mx_kscale(k):
    if not WIDE:
        return np.ones(k)
    levels = np.array([10, -10, 5, -5, 0])
    if k % 512:
        return np.exp2(np.random.permutation(np.resize(levels, k // 32))).repeat(32)
    a = np.empty((k // 512, 16))
    for p in range(k // 512):
        a[p, :8] = np.random.permutation(np.resize(levels, 8))
        for g in range(8):
            far = levels[np.abs(levels - a[p, g]) >= 10]
            a[p, g + 8] = far[np.random.randint(len(far))]
    return np.exp2(a.ravel()).repeat(32)


BF16 = ml_dtypes.bfloat16


def bf(x):
    return np.asarray(x, np.float32).astype(BF16)


def f64(x):
    return np.asarray(x).astype(np.float64)


E2M1 = np.array([0.0, 0.5, 1.0, 1.5, 2.0, 3.0, 4.0, 6.0, -0.0, -0.5, -1.0, -1.5, -2.0, -3.0, -4.0, -6.0])


def pack_weight(w, fmt):
    k, n = w.shape
    w = f64(bf(w)).reshape(k // 32, 32, n)
    amax = np.abs(w).max(1)
    if fmt == "e4m3":
        byte = np.frexp(amax)[1] - 1 + 127 - 7
    else:
        mant, ex = np.frexp(amax / 6.0)
        byte = np.where(mant > 0.5, ex, ex - 1) + 127
    byte = np.clip(np.where(amax > 0, byte, 1), 1, 254)
    scaled = (w * np.exp2(127.0 - byte)[:, None, :]).reshape(k, n).astype(np.float32)
    by_word = np.ascontiguousarray(scaled.reshape(k // 512, 128, 4, n).transpose(0, 1, 3, 2))
    if fmt == "e4m3":
        words = by_word.astype(ml_dtypes.float8_e4m3fn).view(np.uint8)
    else:
        c = by_word.astype(ml_dtypes.float4_e2m1fn).view(np.uint8) & 0xF
        words = c[..., 0::2] | (c[..., 1::2] << 4)
    return np.ascontiguousarray(words), np.ascontiguousarray(byte.astype(np.uint8).reshape(k // 512, 16, n))


def unpack_weight(words, scales, fmt):
    g, p, n, _ = words.shape
    if fmt == "e4m3":
        vals = np.ascontiguousarray(words).view(ml_dtypes.float8_e4m3fn).astype(np.float64)
    else:
        nib = np.empty((g, p, n, 4), np.uint8)
        nib[..., 0::2] = words & 0xF
        nib[..., 1::2] = words >> 4
        vals = E2M1[nib]
    vals = vals * np.repeat(np.exp2(scales.astype(np.float64) - 127.0), 8, axis=1)[..., None]
    return vals.transpose(0, 1, 3, 2).reshape(g * 512, n)

def planes(Y):
    n, m = Y.shape
    b = f64(bf(Y)).reshape(n // 32, 32, m)
    amax = np.abs(b).max(1)
    byte = np.clip(np.where(amax > 0, np.frexp(amax)[1] - 1 + 127 - 7, 1), 1, 254)
    codes = (b * np.exp2(127.0 - byte)[:, None, :]).reshape(n, m).astype(np.float32).astype(ml_dtypes.float8_e4m3fn).view(np.uint8)
    words = codes.reshape(n // 512, 128, 4, m).transpose(0, 1, 3, 2)
    return np.ascontiguousarray(words), np.ascontiguousarray(byte.astype(np.uint8).reshape(n // 512, 16, m))


N, D, H, K = 2048, 1024, 1024, 128


def setup_inputs():
    s, u = mx_kscale(D), mx_kscale(D)
    t = mx_kscale(H)
    x = bf(np.random.standard_normal((N, D)) * s)
    p = bf(np.random.standard_normal((N, D)) * u)
    wr_words, wr_scales = pack_weight(np.random.standard_normal((D, K)) / np.sqrt(D) / s[:, None], "e4m3")
    w1_words, w1_scales = pack_weight(np.random.standard_normal((D, H)) / np.sqrt(D) / u[:, None] * t, "e4m3")
    b1 = bf(0.3 * np.random.standard_normal(H) * t)
    w2_words, w2_scales = pack_weight(1.5 * np.random.standard_normal((H, K)) / np.sqrt(H) / t[:, None], "e4m3")
    lam = bf(np.random.uniform(0.3, 0.9, K))
    return {
        "x": x,
        "p": p,
        "wr_words": wr_words,
        "wr_scales": wr_scales,
        "w1_words": w1_words,
        "w1_scales": w1_scales,
        "b1": b1,
        "w2_words": w2_words,
        "w2_scales": w2_scales,
        "lam": lam,
    }


def softmax(v):
    e = np.exp(v - v.max(axis=-1, keepdims=True))
    return e / e.sum(axis=-1, keepdims=True)


def debiased_rewards(x, wr_words, wr_scales, lam):
    r = mxq(f64(x), 1, "e4m3") @ unpack_weight(wr_words, wr_scales, "e4m3")
    return r - f64(lam)[None, :] * r[:, 0:1]


def gate_weights(p, w1_words, w1_scales, b1, w2_words, w2_scales):
    q = np.maximum((mxq(f64(p), 1, "e4m3") @ unpack_weight(w1_words, w1_scales, "e4m3")) + f64(b1), 0.0)
    return softmax(mxq(q, 1, "e4m3") @ unpack_weight(w2_words, w2_scales, "e4m3"))


def core(x, p, wr_words, wr_scales, w1_words, w1_scales, b1, w2_words, w2_scales, lam):
    rd = debiased_rewards(x, wr_words, wr_scales, lam)
    g = gate_weights(p, w1_words, w1_scales, b1, w2_words, w2_scales)
    num_objectives = wr_words.shape[2]
    return num_objectives * g * rd


def reference(x, p, wr_words, wr_scales, w1_words, w1_scales, b1, w2_words, w2_scales, lam):
    R_out = core(x, p, wr_words, wr_scales, w1_words, w1_scales, b1, w2_words, w2_scales, lam)
    words, scales = planes(R_out)
    return R_out, words, scales

@@ -1,0 +1,349 @@
+from contextlib import ExitStack
+
+import concourse.mybir as mybir
+from concourse.masks import make_identity
+
+N, D, H, K = 2048, 1024, 1024, 128
+FLOPS = 2 * N * D * H + 2 * N * D * K + 2 * N * H * K
+
+F32 = mybir.dt.float32
+BF16 = mybir.dt.bfloat16
+I32 = mybir.dt.int32
+U32 = mybir.dt.uint32
+U8 = mybir.dt.uint8
+FP8X4 = mybir.dt.float8_e4m3fn_x4
+ACT = mybir.ActivationFunctionType
+ALU = mybir.AluOpType
+AX = mybir.AxisListType
+
+P = 128
+GROUP = 512
+GROUPS = N // GROUP
+T = 4
+
+
+def tile_armoverbositydebiasedgatedobjectives_x2_kernel(
+    tc, x, p, wr_words, wr_scales, w1_words, w1_scales, b1, w2_words, w2_scales, lam, out_0, out_1, out_2
+):
+    nc = tc.nc
+    with ExitStack() as ctx:
+        keep = ctx.enter_context(tc.tile_pool(name="keep", bufs=1))
+        work = ctx.enter_context(tc.tile_pool(name="work", bufs=3))
+        psum = ctx.enter_context(tc.psum_pool(name="psum", bufs=1))
+        ctx.enter_context(tc.manual_schedule())
+
+        w1s_raw = keep.tile([P, H], U8, name="w1s_raw", align_bytes=64)
+        nc.vector.memset(w1s_raw[:].bitcast(I32), 0)
+        small_s = keep.tile([P, K], U8, name="small_s", align_bytes=64)
+        nc.vector.memset(small_s[:].bitcast(I32), 0)
+        warm = keep.tile([P, 1], F32, name="warm")
+        nc.vector.memset(warm[:], 0.0)
+        warm_out = keep.tile([P, 1], F32, name="warm_out")
+        ident = keep.tile([P, P], F32, name="ident")
+        make_identity(nc, ident[:])
+        lam_row = keep.tile([P, K], BF16, name="lam_row")
+        nc.vector.memset(lam_row[:], 0.0)
+        ones = keep.tile([P, P], BF16, name="ones")
+        nc.vector.memset(ones[:], 1.0)
+
+        raw = {}
+
+        def load(name, src, n, cuts):
+            tile = keep.tile([P, T, D], BF16, name="raw_%s%d" % (name, n), align_bytes=64)
+            rows = src[GROUP * n : GROUP * (n + 1), :].rearrange("(m t) k -> m t k", t=T)
+            for lo, hi in zip(cuts[:-1], cuts[1:]):
+                ts = slice(lo, hi)
+                nc.sync.dma_start(out=tile[:, ts, :], in_=rows[:, ts, :])
+            raw[name, n] = tile
+
+        w1_raw = []
+
+        def load_w1(hh):
+            tile = keep.tile([P, 2, GROUP], U32, name="w1_raw%d" % hh, align_bytes=64)
+            words = w1_words.rearrange("g p n t -> g p (n t)")[:, :, 2048 * hh : 2048 * (hh + 1)]
+            nc.sync.dma_start(out=tile[:].bitcast(I32), in_=words.bitcast(I32).rearrange("g p n -> p g n"))
+            w1_raw.append(tile)
+
+        def load_small_words(src, name):
+            tile = keep.tile([P, 2, K], U32, name=name, align_bytes=64)
+            words = src.rearrange("g p n t -> g p (n t)").bitcast(I32)
+            nc.sync.dma_start(out=tile[:].bitcast(I32), in_=words.rearrange("g p n -> p g n"))
+            return tile
+
+        for Q in range(4):
+            nc.scalar.dma_start(
+                out=w1s_raw[32 * Q : 32 * Q + 8, :].bitcast(I32), in_=w1_scales[:, 4 * Q : 4 * Q + 4, :].bitcast(I32)
+            )
+        nc.scalar.activation(out=warm_out[:], in_=warm[:], func=ACT.Exp)
+        load("p", p, 0, (0, 1, 2, T))
+        load_w1(0)
+        load_w1(1)
+        b1_bf = keep.tile([P, 2, T], BF16, name="b1_bf")
+        nc.gpsimd.dma_start(out=b1_bf[:], in_=b1.rearrange("(h p t) -> p h t", h=2, t=T))
+        nc.gpsimd.dma_start(out=lam_row[0:1, :], in_=lam.rearrange("(o k) -> o k", o=1))
+        load("p", p, 1, (0, T))
+        load("x", x, 0, (0, T))
+        wr_c = load_small_words(wr_words, "wr_c")
+        w2_c = load_small_words(w2_words, "w2_c")
+        for k0, src in ((0, wr_scales), (8, w2_scales)):
+            for Q in range(4):
+                nc.sync.dma_start(
+                    out=small_s[32 * Q + k0 : 32 * Q + k0 + 8, :].bitcast(I32),
+                    in_=src[:, 4 * Q : 4 * Q + 4, :].bitcast(I32),
+                )
+        load("p", p, 2, (0, T))
+        load("x", x, 1, (0, T))
+        load("p", p, 3, (0, T))
+        load("x", x, 2, (0, T))
+        load("x", x, 3, (0, T))
+
+        w1_c = []
+        w1_s = keep.tile([P, H], U8, name="w1_s", align_bytes=64)
+
+        def permute_w1(hh):
+            tile = keep.tile([P, 2, GROUP], U32, name="w1_c%d" % hh, align_bytes=64)
+            for g in range(2):
+                nc.vector.tensor_copy(
+                    out=tile[:, g, :].bitcast(I32).rearrange("p (t m) -> p t m", t=T),
+                    in_=w1_raw[hh][:, g, :].bitcast(I32).rearrange("p (m t) -> p t m", t=T),
+                )
+            w1_c.append(tile)
+
+        def permute_w1_scales(hh):
+            cols = slice(GROUP * hh, GROUP * (hh + 1))
+            nc.vector.tensor_copy(
+                out=w1_s[:, cols].rearrange("p (t m) -> p t m", t=T),
+                in_=w1s_raw[:, cols].rearrange("p (m t) -> p t m", t=T),
+            )
+
+        grouped, codes, scales = {}, {}, {}
+
+        def drain(engine, out, in_):
+            if engine == "S":
+                nc.scalar.copy(out=out, in_=in_)
+            else:
+                nc.vector.tensor_copy(out=out, in_=in_)
+
+        def turn(name, n, g, b, engine):
+            if (name, n, g) not in grouped:
+                grouped[name, n, g] = work.tile([P, GROUP, 2], F32, name="grouped", align_bytes=64, bufs=4)
+            bank = psum.tile([P, 2, 2, P], F32, name="bank_t", bufs=3)
+            for i in range(2):
+                words = raw[name, n][:, 2 * b + i, :].bitcast(F32)
+                for u in range(2):
+                    nc.tensor.transpose(bank[:, i, u, :], words[:, 256 * g + u : 256 * (g + 1) : 2], ident[:])
+            dst = grouped[name, n, g][:, 256 * b : 256 * (b + 1), :].rearrange("p (i r) u -> p i r u", i=2)
+            drain(engine, dst, bank[:].rearrange("p i u r -> p i r u"))
+
+        def quantize(name, n, g):
+            c = work.tile([P, GROUP], U32, name="codes_" + name, align_bytes=64, bufs=6)
+            s = work.tile([P, GROUP], U8, name="scales_" + name, align_bytes=64, bufs=6)
+            nc.vector.quantize_mx(
+                out=c[:].bitcast(FP8X4), scales=s[:], in_=grouped[name, n, g][:].rearrange("p r u -> p (r u)").bitcast(BF16)
+            )
+            codes[name, n, g] = c
+            scales[name, n, g] = s
+
+        hid = {}
+
+        def stage1(n, hh, js, engines):
+            if (n, hh) not in hid:
+                hid[n, hh] = work.tile([P, T, GROUP], BF16, name="hid", align_bytes=64, bufs=3)
+            planes = hid[n, hh]
+            for j in js:
+                bank = psum.tile([P, GROUP], F32, name="bank_h", bufs=3)
+                for g in range(2):
+                    cols = slice(P * j, P * (j + 1))
+                    scols = slice(GROUP * hh + P * j, GROUP * hh + P * (j + 1))
+                    nc.tensor.matmul_mx(
+                        out=bank[:],
+                        lhsT=w1_c[hh][:, g, cols].bitcast(FP8X4),
+                        lhsT_scale=w1_s[4 * g : P, scols],
+                        rhs=codes["p", n, g][:].bitcast(FP8X4),
+                        rhs_scale=scales["p", n, g][:],
+                        start=(g == 0),
+                        stop=(g == 1),
+                    )
+                bias = b1_f[:, hh, j : j + 1]
+                if engines[j] == "S":
+                    nc.scalar.activation(out=planes[:, j, :], in_=bank[:], func=ACT.Relu, bias=bias)
+                else:
+                    nc.vector.tensor_scalar(
+                        out=planes[:, j, :], in0=bank[:], scalar1=bias, scalar2=0.0, op0=ALU.add, op1=ALU.max
+                    )
+
+        inter = {}
+
+        def interleave(n, hh):
+            q = work.tile([P, GROUP, T], BF16, name="inter", align_bytes=64, bufs=3)
+            nc.vector.tensor_copy(out=q[:], in_=hid[n, hh][:].rearrange("p t r -> p r t"))
+            inter[n, hh] = q
+
+        def quantize_hidden(n, hh):
+            c = work.tile([P, GROUP], U32, name="codes_q", align_bytes=64, bufs=4)
+            s = work.tile([P, GROUP], U8, name="scales_q", align_bytes=64, bufs=4)
+            nc.vector.quantize_mx(
+                out=c[:].bitcast(FP8X4), scales=s[:], in_=inter[n, hh][:].rearrange("p r t -> p (r t)")
+            )
+            codes["q", n, hh] = c
+            scales["q", n, hh] = s
+
+        banks = {}
+
+        def product(kind, name, n, weights, k0):
+            bank = psum.tile([P, T, K], F32, name="bank_" + kind, bufs=1)
+            banks[kind, n] = bank
+            for t in range(T):
+                cols = slice(P * t, P * (t + 1))
+                for g in range(2):
+                    nc.tensor.matmul_mx(
+                        out=bank[:, t, :],
+                        lhsT=codes[name, n, g][:, cols].bitcast(FP8X4),
+                        lhsT_scale=scales[name, n, g][:, cols],
+                        rhs=weights[:, g, :].bitcast(FP8X4),
+                        rhs_scale=small_s[k0 + 4 * g : P, :],
+                        start=(g == 0),
+                        stop=(g == 1),
+                    )
+
+        rd, neg_max, gate, total, inv, result, result_bf = {}, {}, {}, {}, {}, {}, {}
+
+        def debias(n):
+            rd[n] = work.tile([P, T, K], F32, name="rd", bufs=2)
+            r = banks["r", n]
+            for t in range(T):
+                nc.vector.scalar_tensor_tensor(
+                    out=rd[n][:, t, :], in0=neg_lam[:], scalar=r[:, t, 0:1], in1=r[:, t, :], op0=ALU.mult, op1=ALU.add
+                )
+
+        def row_max(n):
+            neg_max[n] = work.tile([P, T], F32, name="neg_max", bufs=2)
+            nc.vector.tensor_reduce(out=neg_max[n][:], in_=banks["l", n][:], axis=AX.X, op=ALU.max, negate=True)
+
+        def exps(n):
+            gate[n] = work.tile([P, T, K], F32, name="gate", bufs=2)
+            total[n] = work.tile([P, T], F32, name="total", bufs=2)
+            for t in range(T):
+                nc.scalar.activation(
+                    out=gate[n][:, t, :],
+                    in_=banks["l", n][:, t, :],
+                    func=ACT.Exp,
+                    bias=neg_max[n][:, t : t + 1],
+                    accum_out=total[n][:, t : t + 1],
+                )
+
+        def combine(n):
+            scaled = work.tile([P, T], F32, name="scaled", bufs=2)
+            inv[n] = work.tile([P, T], F32, name="inv", bufs=2)
+            nc.vector.tensor_scalar(out=scaled[:], in0=total[n][:], scalar1=1.0 / K, scalar2=None, op0=ALU.mult)
+            nc.vector.reciprocal(out=inv[n][:], in_=scaled[:])
+            result[n] = work.tile([P, T, K], F32, name="result", bufs=2)
+            for t in range(T):
+                nc.vector.scalar_tensor_tensor(
+                    out=result[n][:, t, :],
+                    in0=gate[n][:, t, :],
+                    scalar=inv[n][:, t : t + 1],
+                    in1=rd[n][:, t, :],
+                    op0=ALU.mult,
+                    op1=ALU.mult,
+                )
+            nc.sync.dma_start(
+                out=out_0[GROUP * n : GROUP * (n + 1), :].rearrange("(m t) k -> m t k", t=T), in_=result[n][:]
+            )
+
+        def cast(n):
+            result_bf[n] = work.tile([P, K, T], BF16, name="result_bf", align_bytes=64, bufs=2)
+            nc.vector.tensor_copy(out=result_bf[n][:], in_=result[n][:].rearrange("p t k -> p k t"))
+
+        def planes_out(n):
+            c = work.tile([P, K], U32, name="out_c", align_bytes=64, bufs=2)
+            s = work.tile([P, K], U8, name="out_s", align_bytes=64, bufs=2)
+            nc.vector.quantize_mx(
+                out=c[:].bitcast(FP8X4), scales=s[:], in_=result_bf[n][:].rearrange("p k t -> p (k t)")
+            )
+            nc.sync.dma_start(
+                out=out_1[n].rearrange("p k t -> p (k t)").bitcast(I32), in_=c[:].bitcast(I32)
+            )
+            for Q in range(4):
+                nc.sync.dma_start(
+                    out=out_2[n, 4 * Q : 4 * Q + 4, :].bitcast(I32), in_=s[32 * Q : 32 * Q + 4, :].bitcast(I32)
+                )
+
+        turn("p", 0, 0, 0, "S")
+        turn("p", 0, 1, 0, "S")
+        permute_w1_scales(0)
+        permute_w1(0)
+        turn("p", 0, 0, 1, "S")
+        turn("p", 0, 1, 1, "S")
+        quantize("p", 0, 0)
+        quantize("p", 0, 1)
+        b1_f = keep.tile([P, 2, T], F32, name="b1_f")
+        nc.vector.tensor_copy(out=b1_f[:], in_=b1_bf[:])
+        permute_w1_scales(1)
+        permute_w1(1)
+
+        def turns(name, n, engines):
+            for i in range(4):
+                turn(name, n, i // 2, i % 2, engines[i])
+
+        for n in range(GROUPS):
+            last = n == GROUPS - 1
+            stage1(n, 0, range(T), "SSSS")
+            if n:
+                product("l", "q", n - 1, w2_c, 8)
+            if not last:
+                turns("p", n + 1, "SSSS")
+            if n:
+                product("r", "x", n - 1, wr_c, 0)
+            if last:
+                row_max(n - 1)
+                interleave(n, 0)
+            else:
+                interleave(n, 0)
+                if n:
+                    row_max(n - 1)
+            quantize_hidden(n, 0)
+            if n:
+                debias(n - 1)
+                if not last:
+                    exps(n - 1)
+            if not last:
+                quantize("p", n + 1, 0)
+                quantize("p", n + 1, 1)
+            if last:
+                stage1(n, 1, (0, 1), "SSSS")
+                exps(n - 1)
+                stage1(n, 1, (2, 3), "SSSS")
+            else:
+                stage1(n, 1, range(T), "SSSS")
+            if n:
+                combine(n - 1)
+            if last:
+                cast(n - 1)
+            if n == 0:
+                lam_bank = psum.tile([P, T, K], F32, name="bank_r", bufs=1)
+                nc.tensor.matmul(lam_bank[:, 0, :], lhsT=ones[:], rhs=lam_row[:], start=True, stop=True)
+            turns("x", n, "SSSS")
+            interleave(n, 1)
+            if n == 0:
+                neg_lam = keep.tile([P, K], F32, name="neg_lam")
+                nc.vector.tensor_scalar(out=neg_lam[:], in0=lam_bank[:, 0, :], scalar1=-1.0, scalar2=None, op0=ALU.mult)
+            if n and not last:
+                cast(n - 1)
+            if last:
+                planes_out(n - 1)
+            quantize_hidden(n, 1)
+            if n and not last:
+                planes_out(n - 1)
+            quantize("x", n, 0)
+            quantize("x", n, 1)
+
+        n = GROUPS - 1
+        product("l", "q", n, w2_c, 8)
+        product("r", "x", n, wr_c, 0)
+        row_max(n)
+        exps(n)
+        debias(n)
+        combine(n)
+        cast(n)
+        planes_out(n)

@@ -71,11 +71,11 @@ def tile_armoverbositydebiasedgatedobjectives_x2_kernel(
             return tile
 
         for Q in range(4):
-            nc.scalar.dma_start(
+            nc.sync.dma_start(
                 out=w1s_raw[32 * Q : 32 * Q + 8, :].bitcast(I32), in_=w1_scales[:, 4 * Q : 4 * Q + 4, :].bitcast(I32)
             )
         nc.scalar.activation(out=warm_out[:], in_=warm[:], func=ACT.Exp)
-        load("p", p, 0, (0, 1, 2, T))
+        load("p", p, 0, (0, 2, T))
         load_w1(0)
         load_w1(1)
         b1_bf = keep.tile([P, 2, T], BF16, name="b1_bf")
@@ -174,9 +174,12 @@ def tile_armoverbositydebiasedgatedobjectives_x2_kernel(
 
         inter = {}
 
-        def interleave(n, hh):
+        def interleave(n, hh, cut=GROUP):
             q = work.tile([P, GROUP, T], BF16, name="inter", align_bytes=64, bufs=3)
-            nc.vector.tensor_copy(out=q[:], in_=hid[n, hh][:].rearrange("p t r -> p r t"))
+            src = hid[n, hh][:].rearrange("p t r -> p r t")
+            nc.vector.tensor_copy(out=q[:, :cut, :], in_=src[:, :cut, :])
+            if cut < GROUP:
+                nc.scalar.copy(out=q[:, cut:, :], in_=src[:, cut:, :])
             inter[n, hh] = q
 
         def quantize_hidden(n, hh):
@@ -190,10 +193,14 @@ def tile_armoverbositydebiasedgatedobjectives_x2_kernel(
 
         banks = {}
 
-        def product(kind, name, n, weights, k0):
-            bank = psum.tile([P, T, K], F32, name="bank_" + kind, bufs=1)
-            banks[kind, n] = bank
-            for t in range(T):
+        def product(kind, name, n, weights, k0, tag=None, tiles=(0, T)):
+            if tag is None:
+                tag, nb = "bank_" + kind, 1
+            else:
+                nb = 3
+            bank = psum.tile([P, T, K], F32, name=tag, bufs=nb)
+            for t in range(*tiles):
+                banks[kind, n, t] = bank
                 cols = slice(P * t, P * (t + 1))
                 for g in range(2):
                     nc.tensor.matmul_mx(
@@ -210,35 +217,42 @@ def tile_armoverbositydebiasedgatedobjectives_x2_kernel(
 
         def debias(n):
             rd[n] = work.tile([P, T, K], F32, name="rd", bufs=2)
-            r = banks["r", n]
             for t in range(T):
+                r = banks["r", n, t]
                 nc.vector.scalar_tensor_tensor(
                     out=rd[n][:, t, :], in0=neg_lam[:], scalar=r[:, t, 0:1], in1=r[:, t, :], op0=ALU.mult, op1=ALU.add
                 )
 
-        def row_max(n):
-            neg_max[n] = work.tile([P, T], F32, name="neg_max", bufs=2)
-            nc.vector.tensor_reduce(out=neg_max[n][:], in_=banks["l", n][:], axis=AX.X, op=ALU.max, negate=True)
+        def row_max(n, tiles=(0, T)):
+            if n not in neg_max:
+                neg_max[n] = work.tile([P, T], F32, name="neg_max", bufs=2)
+            ts = slice(*tiles)
+            nc.vector.tensor_reduce(
+                out=neg_max[n][:, ts], in_=banks["l", n, tiles[0]][:, ts, :], axis=AX.X, op=ALU.max, negate=True
+            )
 
-        def exps(n):
-            gate[n] = work.tile([P, T, K], F32, name="gate", bufs=2)
-            total[n] = work.tile([P, T], F32, name="total", bufs=2)
-            for t in range(T):
+        def exps(n, tiles=(0, T)):
+            if n not in gate:
+                gate[n] = work.tile([P, T, K], F32, name="gate", bufs=2)
+                total[n] = work.tile([P, T], F32, name="total", bufs=2)
+            for t in range(*tiles):
                 nc.scalar.activation(
                     out=gate[n][:, t, :],
-                    in_=banks["l", n][:, t, :],
+                    in_=banks["l", n, t][:, t, :],
                     func=ACT.Exp,
                     bias=neg_max[n][:, t : t + 1],
                     accum_out=total[n][:, t : t + 1],
                 )
 
-        def combine(n):
+        def combine(n, tiles=(0, T)):
             scaled = work.tile([P, T], F32, name="scaled", bufs=2)
             inv[n] = work.tile([P, T], F32, name="inv", bufs=2)
-            nc.vector.tensor_scalar(out=scaled[:], in0=total[n][:], scalar1=1.0 / K, scalar2=None, op0=ALU.mult)
-            nc.vector.reciprocal(out=inv[n][:], in_=scaled[:])
-            result[n] = work.tile([P, T, K], F32, name="result", bufs=2)
-            for t in range(T):
+            ts = slice(*tiles)
+            nc.vector.tensor_scalar(out=scaled[:, ts], in0=total[n][:, ts], scalar1=1.0 / K, scalar2=None, op0=ALU.mult)
+            nc.vector.reciprocal(out=inv[n][:, ts], in_=scaled[:, ts])
+            if n not in result:
+                result[n] = work.tile([P, T, K], F32, name="result", bufs=2)
+            for t in range(*tiles):
                 nc.vector.scalar_tensor_tensor(
                     out=result[n][:, t, :],
                     in0=gate[n][:, t, :],
@@ -247,9 +261,8 @@ def tile_armoverbositydebiasedgatedobjectives_x2_kernel(
                     op0=ALU.mult,
                     op1=ALU.mult,
                 )
-            nc.sync.dma_start(
-                out=out_0[GROUP * n : GROUP * (n + 1), :].rearrange("(m t) k -> m t k", t=T), in_=result[n][:]
-            )
+            rows = out_0[GROUP * n : GROUP * (n + 1), :].rearrange("(m t) k -> m t k", t=T)
+            nc.sync.dma_start(out=rows[:, ts, :], in_=result[n][:, ts, :])
 
         def cast(n):
             result_bf[n] = work.tile([P, K, T], BF16, name="result_bf", align_bytes=64, bufs=2)
@@ -282,68 +295,70 @@ def tile_armoverbositydebiasedgatedobjectives_x2_kernel(
         permute_w1_scales(1)
         permute_w1(1)
 
-        def turns(name, n, engines):
-            for i in range(4):
-                turn(name, n, i // 2, i % 2, engines[i])
+        def turns(name, n, g, engines="SS"):
+            for b in range(2):
+                turn(name, n, g, b, engines[b])
 
         for n in range(GROUPS):
             last = n == GROUPS - 1
-            stage1(n, 0, range(T), "SSSS")
+            nxt = ("x", n) if last else ("p", n + 1)
+            stage1(n, 0, (0, 1), "SSSS")
+            if n:
+                turns("x", n - 1, 1)
+                quantize("x", n - 1, 1)
+            stage1(n, 0, (2, 3), "SSSS")
             if n:
                 product("l", "q", n - 1, w2_c, 8)
-            if not last:
-                turns("p", n + 1, "SSSS")
+            turns(*nxt, 0)
+            interleave(n, 0)
             if n:
-                product("r", "x", n - 1, wr_c, 0)
-            if last:
                 row_max(n - 1)
-                interleave(n, 0)
-            else:
-                interleave(n, 0)
-                if n:
-                    row_max(n - 1)
+            quantize(*nxt, 0)
             quantize_hidden(n, 0)
+            stage1(n, 1, (0, 1), "SSSS")
             if n:
-                debias(n - 1)
-                if not last:
-                    exps(n - 1)
-            if not last:
-                quantize("p", n + 1, 0)
-                quantize("p", n + 1, 1)
-            if last:
-                stage1(n, 1, (0, 1), "SSSS")
                 exps(n - 1)
-                stage1(n, 1, (2, 3), "SSSS")
-            else:
-                stage1(n, 1, range(T), "SSSS")
-            if n:
-                combine(n - 1)
             if last:
-                cast(n - 1)
+                product("r", "x", n - 1, wr_c, 0)
+            turns(*nxt, 1)
+            if last:
+                debias(n - 1)
+                combine(n - 1)
+            quantize(*nxt, 1)
             if n == 0:
                 lam_bank = psum.tile([P, T, K], F32, name="bank_r", bufs=1)
                 nc.tensor.matmul(lam_bank[:, 0, :], lhsT=ones[:], rhs=lam_row[:], start=True, stop=True)
-            turns("x", n, "SSSS")
-            interleave(n, 1)
-            if n == 0:
                 neg_lam = keep.tile([P, K], F32, name="neg_lam")
                 nc.vector.tensor_scalar(out=neg_lam[:], in0=lam_bank[:, 0, :], scalar1=-1.0, scalar2=None, op0=ALU.mult)
+            stage1(n, 1, (2, 3), "SSSS")
             if n and not last:
-                cast(n - 1)
+                product("r", "x", n - 1, wr_c, 0)
+            if not last:
+                turns("x", n, 0)
+            interleave(n, 1, 320 if last else GROUP)
+            if n and not last:
+                debias(n - 1)
             if last:
-                planes_out(n - 1)
+                cast(n - 1)
+            else:
+                quantize("x", n, 0)
             quantize_hidden(n, 1)
             if n and not last:
+                combine(n - 1)
+                cast(n - 1)
                 planes_out(n - 1)
-            quantize("x", n, 0)
-            quantize("x", n, 1)
 
         n = GROUPS - 1
-        product("l", "q", n, w2_c, 8)
         product("r", "x", n, wr_c, 0)
-        row_max(n)
-        exps(n)
+        product("l", "q", n, w2_c, 8, "bank_h", (0, 2))
+        product("l", "q", n, w2_c, 8, "bank_h", (2, 4))
+        planes_out(n - 1)
         debias(n)
-        combine(n)
+        row_max(n, (0, 2))
+        exps(n, (0, 2))
+        row_max(n, (2, 4))
+        exps(n, (2, 4))
+        combine(n, (0, 2))
+        combine(n, (2, 4))
         cast(n)
         planes_out(n)

@@ -20,6 +20,16 @@ P = 128
 GROUP = 512
 GROUPS = N // GROUP
 T = 4
+HALF = GROUP // 2
+WARM = (2, 0)
+CUT = 96
+STRAIGHT = {("p", 1, 0), ("p", 1, 1), ("x", 0, 1), ("x", 1, 1), ("x", 2, 1)}
+E_P0 = "SS"
+E_P1 = "SS"
+E_X0 = "SS"
+E_X1 = "SS"
+E_A = "SSSS"
+E_B = "SSSS"
 
 
 def tile_armoverbositydebiasedgatedobjectives_x2_kernel(
@@ -43,6 +53,8 @@ def tile_armoverbositydebiasedgatedobjectives_x2_kernel(
         make_identity(nc, ident[:])
         lam_row = keep.tile([P, K], BF16, name="lam_row")
         nc.vector.memset(lam_row[:], 0.0)
+        zeros = keep.tile([P, GROUP], BF16, name="zeros")
+        nc.gpsimd.memset(zeros[:], 0.0)
         ones = keep.tile([P, P], BF16, name="ones")
         nc.vector.memset(ones[:], 1.0)
 
@@ -71,7 +83,7 @@ def tile_armoverbositydebiasedgatedobjectives_x2_kernel(
             return tile
 
         for Q in range(4):
-            nc.sync.dma_start(
+            nc.scalar.dma_start(
                 out=w1s_raw[32 * Q : 32 * Q + 8, :].bitcast(I32), in_=w1_scales[:, 4 * Q : 4 * Q + 4, :].bitcast(I32)
             )
         nc.scalar.activation(out=warm_out[:], in_=warm[:], func=ACT.Exp)
@@ -124,6 +136,16 @@ def tile_armoverbositydebiasedgatedobjectives_x2_kernel(
             else:
                 nc.vector.tensor_copy(out=out, in_=in_)
 
+        flat = {}
+
+        def straighten(name, n, g):
+            if (name, n, g) not in STRAIGHT:
+                return
+            tile = work.tile([P, T, 2, P], F32, name="flat", bufs=3)
+            words = raw[name, n][:].bitcast(F32)[:, :, 256 * g : 256 * (g + 1)]
+            nc.vector.tensor_copy(out=tile[:], in_=words.rearrange("m t (w u) -> m t u w", u=2))
+            flat[name, n, g] = tile
+
         def turn(name, n, g, b, engine):
             if (name, n, g) not in grouped:
                 grouped[name, n, g] = work.tile([P, GROUP, 2], F32, name="grouped", align_bytes=64, bufs=4)
@@ -131,7 +153,11 @@ def tile_armoverbositydebiasedgatedobjectives_x2_kernel(
             for i in range(2):
                 words = raw[name, n][:, 2 * b + i, :].bitcast(F32)
                 for u in range(2):
-                    nc.tensor.transpose(bank[:, i, u, :], words[:, 256 * g + u : 256 * (g + 1) : 2], ident[:])
+                    if (name, n, g) in flat:
+                        block = flat[name, n, g][:, 2 * b + i, u, :]
+                    else:
+                        block = words[:, 256 * g + u : 256 * (g + 1) : 2]
+                    nc.tensor.transpose(bank[:, i, u, :], block, ident[:])
             dst = grouped[name, n, g][:, 256 * b : 256 * (b + 1), :].rearrange("p (i r) u -> p i r u", i=2)
             drain(engine, dst, bank[:].rearrange("p i u r -> p i r u"))
 
@@ -172,24 +198,61 @@ def tile_armoverbositydebiasedgatedobjectives_x2_kernel(
                         out=planes[:, j, :], in0=bank[:], scalar1=bias, scalar2=0.0, op0=ALU.add, op1=ALU.max
                     )
 
+        def stage1_half(n, hh, half, pairs, engines):
+            if (n, hh) not in hid:
+                hid[n, hh] = work.tile([P, T, GROUP], BF16, name="hid", align_bytes=64, bufs=3)
+            rows = slice(HALF * half, HALF * (half + 1))
+            for pair in pairs:
+                bank = psum.tile([P, 2, HALF], F32, name="bank_h", bufs=3)
+                for i in range(2):
+                    j = 2 * pair + i
+                    for g in range(2):
+                        cols = slice(P * j, P * (j + 1))
+                        scols = slice(GROUP * hh + P * j, GROUP * hh + P * (j + 1))
+                        nc.tensor.matmul_mx(
+                            out=bank[:, i, :],
+                            lhsT=w1_c[hh][:, g, cols].bitcast(FP8X4),
+                            lhsT_scale=w1_s[4 * g : P, scols],
+                            rhs=codes["p", n, g][:, rows].bitcast(FP8X4),
+                            rhs_scale=scales["p", n, g][:, rows],
+                            start=(g == 0),
+                            stop=(g == 1),
+                        )
+                for i in range(2):
+                    j = 2 * pair + i
+                    bias = b1_f[:, hh, j : j + 1]
+                    out = hid[n, hh][:, j, rows]
+                    if engines[pair] == "S":
+                        nc.scalar.activation(out=out, in_=bank[:, i, :], func=ACT.Relu, bias=bias)
+                    else:
+                        nc.vector.tensor_scalar(
+                            out=out, in0=bank[:, i, :], scalar1=bias, scalar2=0.0, op0=ALU.add, op1=ALU.max
+                        )
+
         inter = {}
 
-        def interleave(n, hh, cut=GROUP):
-            q = work.tile([P, GROUP, T], BF16, name="inter", align_bytes=64, bufs=3)
+        def interleave(n, hh, lo=0, hi=GROUP, cut=None):
+            if (n, hh) not in inter:
+                inter[n, hh] = work.tile([P, GROUP, T], BF16, name="inter", align_bytes=64, bufs=3)
+            q = inter[n, hh]
+            if cut is None:
+                cut = hi
             src = hid[n, hh][:].rearrange("p t r -> p r t")
-            nc.vector.tensor_copy(out=q[:, :cut, :], in_=src[:, :cut, :])
-            if cut < GROUP:
-                nc.scalar.copy(out=q[:, cut:, :], in_=src[:, cut:, :])
-            inter[n, hh] = q
+            nc.vector.tensor_copy(out=q[:, lo:cut, :], in_=src[:, lo:cut, :])
+            if cut < hi:
+                nc.scalar.copy(out=q[:, cut:hi, :], in_=src[:, cut:hi, :])
 
-        def quantize_hidden(n, hh):
-            c = work.tile([P, GROUP], U32, name="codes_q", align_bytes=64, bufs=4)
-            s = work.tile([P, GROUP], U8, name="scales_q", align_bytes=64, bufs=4)
+        def quantize_hidden(n, hh, lo=0, hi=GROUP):
+            if ("q", n, hh) not in codes:
+                codes["q", n, hh] = work.tile([P, GROUP], U32, name="codes_q", align_bytes=64, bufs=4)
+                scales["q", n, hh] = work.tile([P, GROUP], U8, name="scales_q", align_bytes=64, bufs=4)
+            c = codes["q", n, hh]
+            s = scales["q", n, hh]
             nc.vector.quantize_mx(
-                out=c[:].bitcast(FP8X4), scales=s[:], in_=inter[n, hh][:].rearrange("p r t -> p (r t)")
+                out=c[:, lo:hi].bitcast(FP8X4),
+                scales=s[:, lo:hi],
+                in_=inter[n, hh][:, lo:hi, :].rearrange("p r t -> p (r t)"),
             )
-            codes["q", n, hh] = c
-            scales["q", n, hh] = s
 
         banks = {}
 
@@ -264,63 +327,79 @@ def tile_armoverbositydebiasedgatedobjectives_x2_kernel(
             rows = out_0[GROUP * n : GROUP * (n + 1), :].rearrange("(m t) k -> m t k", t=T)
             nc.sync.dma_start(out=rows[:, ts, :], in_=result[n][:, ts, :])
 
-        def cast(n):
+        def cast(n, engine="V"):
             result_bf[n] = work.tile([P, K, T], BF16, name="result_bf", align_bytes=64, bufs=2)
-            nc.vector.tensor_copy(out=result_bf[n][:], in_=result[n][:].rearrange("p t k -> p k t"))
+            drain(engine, result_bf[n][:], result[n][:].rearrange("p t k -> p k t"))
+
+        out_scales = {}
 
         def planes_out(n):
             c = work.tile([P, K], U32, name="out_c", align_bytes=64, bufs=2)
-            s = work.tile([P, K], U8, name="out_s", align_bytes=64, bufs=2)
+            if n % 2 == 0:
+                out_scales[n // 2] = work.tile([P, K], U8, name="out_s", align_bytes=64, bufs=2)
+            s = out_scales[n // 2]
             nc.vector.quantize_mx(
-                out=c[:].bitcast(FP8X4), scales=s[:], in_=result_bf[n][:].rearrange("p k t -> p (k t)")
+                out=c[:].bitcast(FP8X4),
+                scales=s[4 * (n % 2) : P, :],
+                in_=result_bf[n][:].rearrange("p k t -> p (k t)"),
             )
-            nc.sync.dma_start(
-                out=out_1[n].rearrange("p k t -> p (k t)").bitcast(I32), in_=c[:].bitcast(I32)
-            )
-            for Q in range(4):
-                nc.sync.dma_start(
-                    out=out_2[n, 4 * Q : 4 * Q + 4, :].bitcast(I32), in_=s[32 * Q : 32 * Q + 4, :].bitcast(I32)
-                )
+            nc.sync.dma_start(out=out_1[n].rearrange("p k t -> p (k t)").bitcast(I32), in_=c[:].bitcast(I32))
+            if n % 2 == 1:
+                for Q in range(4):
+                    nc.sync.dma_start(
+                        out=out_2[n - 1 : n + 1, 4 * Q : 4 * Q + 4, :].bitcast(I32),
+                        in_=s[32 * Q : 32 * Q + 8, :].bitcast(I32),
+                    )
+
+        def turns(name, n, g, engines="SS"):
+            for b in range(2):
+                turn(name, n, g, b, engines[b])
+
+        def warm_up(count):
+            for i in range(count):
+                bank = psum.tile([P, 512], F32, name="bank_l", bufs=1)
+                nc.tensor.matmul(bank[:], lhsT=ones[:], rhs=zeros[:], start=True, stop=True)
 
         turn("p", 0, 0, 0, "S")
         turn("p", 0, 1, 0, "S")
-        permute_w1_scales(0)
         permute_w1(0)
+        permute_w1_scales(0)
         turn("p", 0, 0, 1, "S")
         turn("p", 0, 1, 1, "S")
+        warm_up(WARM[0])
         quantize("p", 0, 0)
         quantize("p", 0, 1)
         b1_f = keep.tile([P, 2, T], F32, name="b1_f")
         nc.vector.tensor_copy(out=b1_f[:], in_=b1_bf[:])
         permute_w1_scales(1)
         permute_w1(1)
-
-        def turns(name, n, g, engines="SS"):
-            for b in range(2):
-                turn(name, n, g, b, engines[b])
+        straighten("p", 1, 0)
+        straighten("p", 1, 1)
 
         for n in range(GROUPS):
             last = n == GROUPS - 1
             nxt = ("x", n) if last else ("p", n + 1)
-            stage1(n, 0, (0, 1), "SSSS")
+            stage1(n, 0, (0, 1), E_A)
             if n:
-                turns("x", n - 1, 1)
+                turns("x", n - 1, 1, E_X1)
                 quantize("x", n - 1, 1)
-            stage1(n, 0, (2, 3), "SSSS")
+            stage1(n, 0, (2, 3), E_A)
             if n:
                 product("l", "q", n - 1, w2_c, 8)
-            turns(*nxt, 0)
+            turns(*nxt, 0, E_P0)
             interleave(n, 0)
             if n:
                 row_max(n - 1)
             quantize(*nxt, 0)
             quantize_hidden(n, 0)
-            stage1(n, 1, (0, 1), "SSSS")
+            if not last:
+                straighten("x", n, 1)
+            stage1(n, 1, (0, 1), E_B)
             if n:
                 exps(n - 1)
             if last:
                 product("r", "x", n - 1, wr_c, 0)
-            turns(*nxt, 1)
+            turns(*nxt, 1, E_P1)
             if last:
                 debias(n - 1)
                 combine(n - 1)
@@ -330,35 +409,38 @@ def tile_armoverbositydebiasedgatedobjectives_x2_kernel(
                 nc.tensor.matmul(lam_bank[:, 0, :], lhsT=ones[:], rhs=lam_row[:], start=True, stop=True)
                 neg_lam = keep.tile([P, K], F32, name="neg_lam")
                 nc.vector.tensor_scalar(out=neg_lam[:], in0=lam_bank[:, 0, :], scalar1=-1.0, scalar2=None, op0=ALU.mult)
-            stage1(n, 1, (2, 3), "SSSS")
-            if n and not last:
-                product("r", "x", n - 1, wr_c, 0)
             if not last:
-                turns("x", n, 0)
-            interleave(n, 1, 320 if last else GROUP)
-            if n and not last:
-                debias(n - 1)
-            if last:
-                cast(n - 1)
-            else:
+                stage1(n, 1, (2, 3), E_B)
+                if n:
+                    product("r", "x", n - 1, wr_c, 0)
+                turns("x", n, 0, E_X0)
+                straighten(*(("p", n + 2) if n + 2 < GROUPS else ("x", n + 1)), 0)
+                interleave(n, 1)
+                if n:
+                    debias(n - 1)
                 quantize("x", n, 0)
-            quantize_hidden(n, 1)
-            if n and not last:
-                combine(n - 1)
-                cast(n - 1)
-                planes_out(n - 1)
+                quantize_hidden(n, 1)
+                if n:
+                    combine(n - 1)
+                    cast(n - 1)
+                    planes_out(n - 1)
 
-        n = GROUPS - 1
+        stage1_half(n, 1, 0, (1,), "SS")
+        stage1_half(n, 1, 1, (1,), "SS")
         product("r", "x", n, wr_c, 0)
+        interleave(n, 1, 0, HALF)
+        interleave(n, 1, HALF, GROUP, HALF + CUT)
+        cast(n - 1, "S")
+        quantize_hidden(n, 1, 0, HALF)
         product("l", "q", n, w2_c, 8, "bank_h", (0, 2))
-        product("l", "q", n, w2_c, 8, "bank_h", (2, 4))
+        quantize_hidden(n, 1, HALF, GROUP)
         planes_out(n - 1)
-        debias(n)
+        product("l", "q", n, w2_c, 8, "bank_h", (2, 4))
         row_max(n, (0, 2))
         exps(n, (0, 2))
         row_max(n, (2, 4))
+        debias(n)
         exps(n, (2, 4))
-        combine(n, (0, 2))
-        combine(n, (2, 4))
+        combine(n)
         cast(n)
         planes_out(n)

@@ -23,13 +23,120 @@ T = 4
 HALF = GROUP // 2
 WARM = (2, 0)
 CUT = 96
-STRAIGHT = {("p", 1, 0), ("p", 1, 1), ("x", 0, 1), ("x", 1, 1), ("x", 2, 1)}
-E_P0 = "SS"
-E_P1 = "SS"
-E_X0 = "SS"
-E_X1 = "SS"
-E_A = "SSSS"
-E_B = "SSSS"
+NT = 3
+NH = 3
+STRAIGHT = {("p", 1, 0), ("p", 1, 1), ("p", 2, 1), ("p", 3, 0), ("p", 3, 1), ("x", 0, 0), ("x", 0, 1), ("x", 1, 1), ("x", 2, 1)}
+ENG = {("A", 0, 1, 0): "SV", ("T", "p", 3, 0): "SV", ("T", "p", 1, 0): "SV"}
+PROGRAM = [
+    ("st", "p", 1, 0),
+    ("st", "p", 1, 1),
+    ("A", 0, 0, 1),
+    ("A", 0, 0, 0),
+    ("st", "x", 0, 0),
+    ("T", "p", 1, 0),
+    ("Q", "p", 1, 0),
+    ("I", 0, 0, 0, 512, 384),
+    ("A", 0, 1, 0),
+    ("T", "p", 1, 1),
+    ("lam",),
+    ("Q", "p", 1, 1),
+    ("A", 0, 1, 1),
+    ("st", "x", 0, 1),
+    ("T", "x", 0, 0),
+    ("I", 0, 1, 0, 512, 512),
+    ("A", 1, 0, 1),
+    ("QQ", 0, 0),
+    ("T", "x", 0, 1),
+    ("A", 1, 0, 0),
+    ("st", "p", 2, 1),
+    ("QQ", 0, 1),
+    ("Q", "x", 0, 0),
+    ("Q", "x", 0, 1),
+    ("T", "p", 2, 0),
+    ("st", "p", 3, 0),
+    ("S2", 0),
+    ("I", 1, 0, 0, 512, 512),
+    ("max", 0),
+    ("QQ", 1, 0),
+    ("T", "p", 2, 1),
+    ("A", 1, 1, 0),
+    ("Q", "p", 2, 1),
+    ("Q", "p", 2, 0),
+    ("RR", 0),
+    ("exp", 0),
+    ("A", 1, 1, 1),
+    ("st", "x", 1, 1),
+    ("st", "p", 3, 1),
+    ("T", "x", 1, 0),
+    ("rd", 0),
+    ("I", 1, 1, 0, 512, 512),
+    ("A", 2, 0, 0),
+    ("Q", "x", 1, 0),
+    ("T", "x", 1, 1),
+    ("QQ", 1, 1),
+    ("comb", 0),
+    ("A", 2, 0, 1),
+    ("T", "p", 3, 0),
+    ("cast", 0),
+    ("I", 2, 0, 0, 512, 320),
+    ("Q", "p", 3, 0),
+    ("A", 2, 1, 0),
+    ("S2", 1),
+    ("T", "p", 3, 1),
+    ("st", "x", 2, 1),
+    ("max", 1),
+    ("A", 2, 1, 1),
+    ("exp", 1),
+    ("T", "x", 2, 0),
+    ("Q", "x", 1, 1),
+    ("Q", "p", 3, 1),
+    ("QQ", 2, 0),
+    ("I", 2, 1, 0, 512, 512),
+    ("RR", 1),
+    ("A", 3, 0, 1),
+    ("rd", 1),
+    ("T", "x", 2, 1),
+    ("A", 3, 0, 0),
+    ("Ah", 3, 1, 0),
+    ("out", 0),
+    ("QQ", 2, 1),
+    ("S2", 2),
+    ("comb", 1),
+    ("Q", "x", 2, 0),
+    ("Q", "x", 2, 1),
+    ("max", 2),
+    ("I", 3, 0, 0, 512, 448),
+    ("cast", 1),
+    ("T", "x", 3, 0),
+    ("QQ", 3, 0),
+    ("Q", "x", 3, 0),
+    ("RR", 2),
+    ("exp", 2),
+    ("rd", 2),
+    ("comb", 2),
+    ("T", "x", 3, 1),
+    ("Q", "x", 3, 1),
+    ("A", 3, 1, 0),
+    ("Ah", 3, 1, 1),
+    ("I", 3, 1, 0, 256, 192),
+    ("I", 3, 1, 256, 512, 384),
+    ("RR", 3),
+    ("QQ", 3, 1, 0, 256),
+    ("out", 1),
+    ("QQ", 3, 1, 256, 512),
+    ("S2h", 3, 0, 2),
+    ("max", 3, 0, 2),
+    ("S2h", 3, 2, 4),
+    ("max", 3, 2, 4),
+    ("cast", 2, "S"),
+    ("exp", 3, 0, 2),
+    ("exp", 3, 2, 4),
+    ("out", 2),
+    ("rd", 3),
+    ("comb", 3),
+    ("cast", 3),
+    ("out", 3),
+]
 
 
 def tile_armoverbositydebiasedgatedobjectives_x2_kernel(
@@ -149,7 +256,7 @@ def tile_armoverbositydebiasedgatedobjectives_x2_kernel(
         def turn(name, n, g, b, engine):
             if (name, n, g) not in grouped:
                 grouped[name, n, g] = work.tile([P, GROUP, 2], F32, name="grouped", align_bytes=64, bufs=4)
-            bank = psum.tile([P, 2, 2, P], F32, name="bank_t", bufs=3)
+            bank = psum.tile([P, 2, 2, P], F32, name="bank_t", bufs=NT)
             for i in range(2):
                 words = raw[name, n][:, 2 * b + i, :].bitcast(F32)
                 for u in range(2):
@@ -177,7 +284,7 @@ def tile_armoverbositydebiasedgatedobjectives_x2_kernel(
                 hid[n, hh] = work.tile([P, T, GROUP], BF16, name="hid", align_bytes=64, bufs=3)
             planes = hid[n, hh]
             for j in js:
-                bank = psum.tile([P, GROUP], F32, name="bank_h", bufs=3)
+                bank = psum.tile([P, GROUP], F32, name="bank_h", bufs=NH)
                 for g in range(2):
                     cols = slice(P * j, P * (j + 1))
                     scols = slice(GROUP * hh + P * j, GROUP * hh + P * (j + 1))
@@ -203,7 +310,7 @@ def tile_armoverbositydebiasedgatedobjectives_x2_kernel(
                 hid[n, hh] = work.tile([P, T, GROUP], BF16, name="hid", align_bytes=64, bufs=3)
             rows = slice(HALF * half, HALF * (half + 1))
             for pair in pairs:
-                bank = psum.tile([P, 2, HALF], F32, name="bank_h", bufs=3)
+                bank = psum.tile([P, 2, HALF], F32, name="bank_h", bufs=NH)
                 for i in range(2):
                     j = 2 * pair + i
                     for g in range(2):
@@ -237,10 +344,11 @@ def tile_armoverbositydebiasedgatedobjectives_x2_kernel(
             q = inter[n, hh]
             if cut is None:
                 cut = hi
-            src = hid[n, hh][:].rearrange("p t r -> p r t")
-            nc.vector.tensor_copy(out=q[:, lo:cut, :], in_=src[:, lo:cut, :])
+            dst = q[:].rearrange("p (c i) t -> p c t i", i=4)
+            src = hid[n, hh][:].rearrange("p t (c i) -> p c t i", i=4)
+            nc.vector.tensor_copy(out=dst[:, lo // 4 : cut // 4], in_=src[:, lo // 4 : cut // 4])
             if cut < hi:
-                nc.scalar.copy(out=q[:, cut:hi, :], in_=src[:, cut:hi, :])
+                nc.scalar.copy(out=dst[:, cut // 4 : hi // 4], in_=src[:, cut // 4 : hi // 4])
 
         def quantize_hidden(n, hh, lo=0, hi=GROUP):
             if ("q", n, hh) not in codes:
@@ -260,7 +368,7 @@ def tile_armoverbositydebiasedgatedobjectives_x2_kernel(
             if tag is None:
                 tag, nb = "bank_" + kind, 1
             else:
-                nb = 3
+                nb = NH
             bank = psum.tile([P, T, K], F32, name=tag, bufs=nb)
             for t in range(*tiles):
                 banks[kind, n, t] = bank
@@ -286,7 +394,8 @@ def tile_armoverbositydebiasedgatedobjectives_x2_kernel(
                     out=rd[n][:, t, :], in0=neg_lam[:], scalar=r[:, t, 0:1], in1=r[:, t, :], op0=ALU.mult, op1=ALU.add
                 )
 
-        def row_max(n, tiles=(0, T)):
+        def row_max(n, lo=0, hi=T):
+            tiles = (lo, hi)
             if n not in neg_max:
                 neg_max[n] = work.tile([P, T], F32, name="neg_max", bufs=2)
             ts = slice(*tiles)
@@ -294,7 +403,8 @@ def tile_armoverbositydebiasedgatedobjectives_x2_kernel(
                 out=neg_max[n][:, ts], in_=banks["l", n, tiles[0]][:, ts, :], axis=AX.X, op=ALU.max, negate=True
             )
 
-        def exps(n, tiles=(0, T)):
+        def exps(n, lo=0, hi=T):
+            tiles = (lo, hi)
             if n not in gate:
                 gate[n] = work.tile([P, T, K], F32, name="gate", bufs=2)
                 total[n] = work.tile([P, T], F32, name="total", bufs=2)
@@ -373,74 +483,31 @@ def tile_armoverbositydebiasedgatedobjectives_x2_kernel(
         nc.vector.tensor_copy(out=b1_f[:], in_=b1_bf[:])
         permute_w1_scales(1)
         permute_w1(1)
-        straighten("p", 1, 0)
-        straighten("p", 1, 1)
 
-        for n in range(GROUPS):
-            last = n == GROUPS - 1
-            nxt = ("x", n) if last else ("p", n + 1)
-            stage1(n, 0, (0, 1), E_A)
-            if n:
-                turns("x", n - 1, 1, E_X1)
-                quantize("x", n - 1, 1)
-            stage1(n, 0, (2, 3), E_A)
-            if n:
-                product("l", "q", n - 1, w2_c, 8)
-            turns(*nxt, 0, E_P0)
-            interleave(n, 0)
-            if n:
-                row_max(n - 1)
-            quantize(*nxt, 0)
-            quantize_hidden(n, 0)
-            if not last:
-                straighten("x", n, 1)
-            stage1(n, 1, (0, 1), E_B)
-            if n:
-                exps(n - 1)
-            if last:
-                product("r", "x", n - 1, wr_c, 0)
-            turns(*nxt, 1, E_P1)
-            if last:
-                debias(n - 1)
-                combine(n - 1)
-            quantize(*nxt, 1)
-            if n == 0:
-                lam_bank = psum.tile([P, T, K], F32, name="bank_r", bufs=1)
-                nc.tensor.matmul(lam_bank[:, 0, :], lhsT=ones[:], rhs=lam_row[:], start=True, stop=True)
-                neg_lam = keep.tile([P, K], F32, name="neg_lam")
-                nc.vector.tensor_scalar(out=neg_lam[:], in0=lam_bank[:, 0, :], scalar1=-1.0, scalar2=None, op0=ALU.mult)
-            if not last:
-                stage1(n, 1, (2, 3), E_B)
-                if n:
-                    product("r", "x", n - 1, wr_c, 0)
-                turns("x", n, 0, E_X0)
-                straighten(*(("p", n + 2) if n + 2 < GROUPS else ("x", n + 1)), 0)
-                interleave(n, 1)
-                if n:
-                    debias(n - 1)
-                quantize("x", n, 0)
-                quantize_hidden(n, 1)
-                if n:
-                    combine(n - 1)
-                    cast(n - 1)
-                    planes_out(n - 1)
+        def lam_prep():
+            lam_bank = psum.tile([P, T, K], F32, name="bank_r", bufs=1)
+            nc.tensor.matmul(lam_bank[:, 0, :], lhsT=ones[:], rhs=lam_row[:], start=True, stop=True)
+            nc.vector.tensor_scalar(out=neg_lam[:], in0=lam_bank[:, 0, :], scalar1=-1.0, scalar2=None, op0=ALU.mult)
 
-        stage1_half(n, 1, 0, (1,), "SS")
-        stage1_half(n, 1, 1, (1,), "SS")
-        product("r", "x", n, wr_c, 0)
-        interleave(n, 1, 0, HALF)
-        interleave(n, 1, HALF, GROUP, HALF + CUT)
-        cast(n - 1, "S")
-        quantize_hidden(n, 1, 0, HALF)
-        product("l", "q", n, w2_c, 8, "bank_h", (0, 2))
-        quantize_hidden(n, 1, HALF, GROUP)
-        planes_out(n - 1)
-        product("l", "q", n, w2_c, 8, "bank_h", (2, 4))
-        row_max(n, (0, 2))
-        exps(n, (0, 2))
-        row_max(n, (2, 4))
-        debias(n)
-        exps(n, (2, 4))
-        combine(n)
-        cast(n)
-        planes_out(n)
+        neg_lam = keep.tile([P, K], F32, name="neg_lam")
+        steps = {
+            "T": lambda name, n, g: turns(name, n, g, ENG.get(("T", name, n, g), "SS")),
+            "A": lambda n, hh, pair: stage1(n, hh, (2 * pair, 2 * pair + 1), ENG.get(("A", n, hh, pair), "SS") * 2),
+            "Ah": lambda n, hh, half: stage1_half(n, hh, half, (1,), "SS"),
+            "Q": quantize,
+            "st": straighten,
+            "I": interleave,
+            "QQ": quantize_hidden,
+            "RR": lambda n: product("r", "x", n, wr_c, 0),
+            "S2": lambda n: product("l", "q", n, w2_c, 8),
+            "S2h": lambda n, lo, hi: product("l", "q", n, w2_c, 8, "bank_h", (lo, hi)),
+            "max": row_max,
+            "exp": exps,
+            "rd": debias,
+            "comb": combine,
+            "cast": cast,
+            "out": planes_out,
+            "lam": lam_prep,
+        }
+        for step in PROGRAM:
+            steps[step[0]](*step[1:])

@@ -17,126 +17,13 @@ ALU = mybir.AluOpType
 AX = mybir.AxisListType
 
 P = 128
-GROUP = 512
-GROUPS = N // GROUP
-T = 4
+PACK = 4
+GROUP = P * PACK
 HALF = GROUP // 2
-WARM = (2, 0)
-CUT = 96
-NT = 3
-NH = 3
-STRAIGHT = {("p", 1, 0), ("p", 1, 1), ("p", 2, 1), ("p", 3, 0), ("p", 3, 1), ("x", 0, 0), ("x", 0, 1), ("x", 1, 1), ("x", 2, 1)}
-ENG = {("A", 0, 1, 0): "SV", ("T", "p", 3, 0): "SV", ("T", "p", 1, 0): "SV"}
-PROGRAM = [
-    ("st", "p", 1, 0),
-    ("st", "p", 1, 1),
-    ("A", 0, 0, 1),
-    ("A", 0, 0, 0),
-    ("st", "x", 0, 0),
-    ("T", "p", 1, 0),
-    ("Q", "p", 1, 0),
-    ("I", 0, 0, 0, 512, 384),
-    ("A", 0, 1, 0),
-    ("T", "p", 1, 1),
-    ("lam",),
-    ("Q", "p", 1, 1),
-    ("A", 0, 1, 1),
-    ("st", "x", 0, 1),
-    ("T", "x", 0, 0),
-    ("I", 0, 1, 0, 512, 512),
-    ("A", 1, 0, 1),
-    ("QQ", 0, 0),
-    ("T", "x", 0, 1),
-    ("A", 1, 0, 0),
-    ("st", "p", 2, 1),
-    ("QQ", 0, 1),
-    ("Q", "x", 0, 0),
-    ("Q", "x", 0, 1),
-    ("T", "p", 2, 0),
-    ("st", "p", 3, 0),
-    ("S2", 0),
-    ("I", 1, 0, 0, 512, 512),
-    ("max", 0),
-    ("QQ", 1, 0),
-    ("T", "p", 2, 1),
-    ("A", 1, 1, 0),
-    ("Q", "p", 2, 1),
-    ("Q", "p", 2, 0),
-    ("RR", 0),
-    ("exp", 0),
-    ("A", 1, 1, 1),
-    ("st", "x", 1, 1),
-    ("st", "p", 3, 1),
-    ("T", "x", 1, 0),
-    ("rd", 0),
-    ("I", 1, 1, 0, 512, 512),
-    ("A", 2, 0, 0),
-    ("Q", "x", 1, 0),
-    ("T", "x", 1, 1),
-    ("QQ", 1, 1),
-    ("comb", 0),
-    ("A", 2, 0, 1),
-    ("T", "p", 3, 0),
-    ("cast", 0),
-    ("I", 2, 0, 0, 512, 320),
-    ("Q", "p", 3, 0),
-    ("A", 2, 1, 0),
-    ("S2", 1),
-    ("T", "p", 3, 1),
-    ("st", "x", 2, 1),
-    ("max", 1),
-    ("A", 2, 1, 1),
-    ("exp", 1),
-    ("T", "x", 2, 0),
-    ("Q", "x", 1, 1),
-    ("Q", "p", 3, 1),
-    ("QQ", 2, 0),
-    ("I", 2, 1, 0, 512, 512),
-    ("RR", 1),
-    ("A", 3, 0, 1),
-    ("rd", 1),
-    ("T", "x", 2, 1),
-    ("A", 3, 0, 0),
-    ("Ah", 3, 1, 0),
-    ("out", 0),
-    ("QQ", 2, 1),
-    ("S2", 2),
-    ("comb", 1),
-    ("Q", "x", 2, 0),
-    ("Q", "x", 2, 1),
-    ("max", 2),
-    ("I", 3, 0, 0, 512, 448),
-    ("cast", 1),
-    ("T", "x", 3, 0),
-    ("QQ", 3, 0),
-    ("Q", "x", 3, 0),
-    ("RR", 2),
-    ("exp", 2),
-    ("rd", 2),
-    ("comb", 2),
-    ("T", "x", 3, 1),
-    ("Q", "x", 3, 1),
-    ("A", 3, 1, 0),
-    ("Ah", 3, 1, 1),
-    ("I", 3, 1, 0, 256, 192),
-    ("I", 3, 1, 256, 512, 384),
-    ("RR", 3),
-    ("QQ", 3, 1, 0, 256),
-    ("out", 1),
-    ("QQ", 3, 1, 256, 512),
-    ("S2h", 3, 0, 2),
-    ("max", 3, 0, 2),
-    ("S2h", 3, 2, 4),
-    ("max", 3, 2, 4),
-    ("cast", 2, "S"),
-    ("exp", 3, 0, 2),
-    ("exp", 3, 2, 4),
-    ("out", 2),
-    ("rd", 3),
-    ("comb", 3),
-    ("cast", 3),
-    ("out", 3),
-]
+GROUPS = N // GROUP
+PASSES = 2
+TILES = GROUP // P
+SCALE_ROWS = 4
 
 
 def tile_armoverbositydebiasedgatedobjectives_x2_kernel(
@@ -145,369 +32,416 @@ def tile_armoverbositydebiasedgatedobjectives_x2_kernel(
     nc = tc.nc
     with ExitStack() as ctx:
         keep = ctx.enter_context(tc.tile_pool(name="keep", bufs=1))
-        work = ctx.enter_context(tc.tile_pool(name="work", bufs=3))
+        work = ctx.enter_context(tc.tile_pool(name="work", bufs=2))
         psum = ctx.enter_context(tc.psum_pool(name="psum", bufs=1))
         ctx.enter_context(tc.manual_schedule())
 
-        w1s_raw = keep.tile([P, H], U8, name="w1s_raw", align_bytes=64)
-        nc.vector.memset(w1s_raw[:].bitcast(I32), 0)
-        small_s = keep.tile([P, K], U8, name="small_s", align_bytes=64)
-        nc.vector.memset(small_s[:].bitcast(I32), 0)
-        warm = keep.tile([P, 1], F32, name="warm")
-        nc.vector.memset(warm[:], 0.0)
-        warm_out = keep.tile([P, 1], F32, name="warm_out")
-        ident = keep.tile([P, P], F32, name="ident")
-        make_identity(nc, ident[:])
+        w1_raw_scales = keep.tile([P, H], U8, name="w1_raw_scales", align_bytes=64)
+        nc.vector.memset(w1_raw_scales[:].bitcast(I32), 0)
+        small_scales = keep.tile([P, K], U8, name="small_scales", align_bytes=64)
+        nc.vector.memset(small_scales[:].bitcast(I32), 0)
+        wr_row, w2_row = 0, PASSES * SCALE_ROWS
+
+        zero = keep.tile([P, P], BF16, name="zero")
+        nc.vector.memset(zero[:], 0.0)
+        identity = keep.tile([P, P], F32, name="identity")
+        make_identity(nc, identity[:])
         lam_row = keep.tile([P, K], BF16, name="lam_row")
         nc.vector.memset(lam_row[:], 0.0)
-        zeros = keep.tile([P, GROUP], BF16, name="zeros")
-        nc.gpsimd.memset(zeros[:], 0.0)
-        ones = keep.tile([P, P], BF16, name="ones")
-        nc.vector.memset(ones[:], 1.0)
+
+        def load_scales(queue, tile, scales, first_row):
+            for quadrant in range(4):
+                first = 32 * quadrant + first_row
+                queue.dma_start(
+                    out=tile[first : first + PASSES * SCALE_ROWS, :].bitcast(I32),
+                    in_=scales[:, SCALE_ROWS * quadrant : SCALE_ROWS * (quadrant + 1), :].bitcast(I32),
+                )
 
         raw = {}
 
-        def load(name, src, n, cuts):
-            tile = keep.tile([P, T, D], BF16, name="raw_%s%d" % (name, n), align_bytes=64)
-            rows = src[GROUP * n : GROUP * (n + 1), :].rearrange("(m t) k -> m t k", t=T)
-            for lo, hi in zip(cuts[:-1], cuts[1:]):
-                ts = slice(lo, hi)
-                nc.sync.dma_start(out=tile[:, ts, :], in_=rows[:, ts, :])
-            raw[name, n] = tile
+        def load(name, source, n, lo=0, hi=TILES):
+            if (name, n) not in raw:
+                raw[name, n] = keep.tile([P, TILES, D], BF16, name="raw_%s%d" % (name, n), align_bytes=64)
+            rows = source[GROUP * n : GROUP * (n + 1), :].rearrange("(m t) k -> m t k", t=TILES)
+            nc.sync.dma_start(out=raw[name, n][:, lo:hi, :], in_=rows[:, lo:hi, :])
 
-        w1_raw = []
-
-        def load_w1(hh):
-            tile = keep.tile([P, 2, GROUP], U32, name="w1_raw%d" % hh, align_bytes=64)
-            words = w1_words.rearrange("g p n t -> g p (n t)")[:, :, 2048 * hh : 2048 * (hh + 1)]
-            nc.sync.dma_start(out=tile[:].bitcast(I32), in_=words.bitcast(I32).rearrange("g p n -> p g n"))
-            w1_raw.append(tile)
-
-        def load_small_words(src, name):
-            tile = keep.tile([P, 2, K], U32, name=name, align_bytes=64)
-            words = src.rearrange("g p n t -> g p (n t)").bitcast(I32)
+        def load_words(source, name, lo, hi):
+            tile = keep.tile([P, PASSES, hi - lo], U32, name=name, align_bytes=64)
+            words = source.rearrange("g p n t -> g p (n t)")[:, :, PACK * lo : PACK * hi].bitcast(I32)
             nc.sync.dma_start(out=tile[:].bitcast(I32), in_=words.rearrange("g p n -> p g n"))
             return tile
 
-        for Q in range(4):
-            nc.scalar.dma_start(
-                out=w1s_raw[32 * Q : 32 * Q + 8, :].bitcast(I32), in_=w1_scales[:, 4 * Q : 4 * Q + 4, :].bitcast(I32)
-            )
-        nc.scalar.activation(out=warm_out[:], in_=warm[:], func=ACT.Exp)
-        load("p", p, 0, (0, 2, T))
-        load_w1(0)
-        load_w1(1)
-        b1_bf = keep.tile([P, 2, T], BF16, name="b1_bf")
-        nc.gpsimd.dma_start(out=b1_bf[:], in_=b1.rearrange("(h p t) -> p h t", h=2, t=T))
+        load_scales(nc.scalar, w1_raw_scales, w1_scales, 0)
+        ones = keep.tile([P, P], BF16, name="ones")
+        nc.scalar.activation(out=ones[:], in_=zero[:], func=ACT.Exp)
+        load("p", p, 0, 0, 2)
+        load("p", p, 0, 2, TILES)
+        w1_raw = [load_words(w1_words, "w1_raw0", 0, GROUP)]
+        w1_raw.append(load_words(w1_words, "w1_raw1", GROUP, H))
         nc.gpsimd.dma_start(out=lam_row[0:1, :], in_=lam.rearrange("(o k) -> o k", o=1))
-        load("p", p, 1, (0, T))
-        load("x", x, 0, (0, T))
-        wr_c = load_small_words(wr_words, "wr_c")
-        w2_c = load_small_words(w2_words, "w2_c")
-        for k0, src in ((0, wr_scales), (8, w2_scales)):
-            for Q in range(4):
-                nc.sync.dma_start(
-                    out=small_s[32 * Q + k0 : 32 * Q + k0 + 8, :].bitcast(I32),
-                    in_=src[:, 4 * Q : 4 * Q + 4, :].bitcast(I32),
-                )
-        load("p", p, 2, (0, T))
-        load("x", x, 1, (0, T))
-        load("p", p, 3, (0, T))
-        load("x", x, 2, (0, T))
-        load("x", x, 3, (0, T))
+        b1_columns = keep.tile([P, 2, PACK], BF16, name="b1_columns")
+        nc.gpsimd.dma_start(out=b1_columns[:], in_=b1.rearrange("(h m j) -> m h j", h=2, j=PACK))
+        load("p", p, 1)
+        load("x", x, 0)
+        wr_codes = load_words(wr_words, "wr_codes", 0, K)
+        w2_codes = load_words(w2_words, "w2_codes", 0, K)
+        load_scales(nc.sync, small_scales, wr_scales, wr_row)
+        load_scales(nc.sync, small_scales, w2_scales, w2_row)
+        load("p", p, 2)
+        load("x", x, 1)
+        load("p", p, 3)
+        load("x", x, 2)
+        load("x", x, 3)
 
-        w1_c = []
-        w1_s = keep.tile([P, H], U8, name="w1_s", align_bytes=64)
+        w1_codes = []
+        w1_scale = keep.tile([P, H], U8, name="w1_scale", align_bytes=64)
 
-        def permute_w1(hh):
-            tile = keep.tile([P, 2, GROUP], U32, name="w1_c%d" % hh, align_bytes=64)
-            for g in range(2):
+        def reorder_w1(h):
+            tile = keep.tile([P, PASSES, GROUP], U32, name="w1_codes%d" % h, align_bytes=64)
+            for g in range(PASSES):
                 nc.vector.tensor_copy(
-                    out=tile[:, g, :].bitcast(I32).rearrange("p (t m) -> p t m", t=T),
-                    in_=w1_raw[hh][:, g, :].bitcast(I32).rearrange("p (m t) -> p t m", t=T),
+                    out=tile[:, g, :].bitcast(I32).rearrange("p (j m) -> p j m", j=PACK),
+                    in_=w1_raw[h][:, g, :].bitcast(I32).rearrange("p (m j) -> p j m", j=PACK),
                 )
-            w1_c.append(tile)
+            w1_codes.append(tile)
 
-        def permute_w1_scales(hh):
-            cols = slice(GROUP * hh, GROUP * (hh + 1))
+        def reorder_w1_scales(h):
+            cols = slice(GROUP * h, GROUP * (h + 1))
             nc.vector.tensor_copy(
-                out=w1_s[:, cols].rearrange("p (t m) -> p t m", t=T),
-                in_=w1s_raw[:, cols].rearrange("p (m t) -> p t m", t=T),
+                out=w1_scale[:, cols].rearrange("p (j m) -> p j m", j=PACK),
+                in_=w1_raw_scales[:, cols].rearrange("p (m j) -> p j m", j=PACK),
             )
 
-        grouped, codes, scales = {}, {}, {}
+        turned, straight, codes, scales = {}, {}, {}, {}
 
-        def drain(engine, out, in_):
+        def move(engine, out, in_):
             if engine == "S":
                 nc.scalar.copy(out=out, in_=in_)
             else:
                 nc.vector.tensor_copy(out=out, in_=in_)
 
-        flat = {}
-
         def straighten(name, n, g):
-            if (name, n, g) not in STRAIGHT:
-                return
-            tile = work.tile([P, T, 2, P], F32, name="flat", bufs=3)
+            tile = work.tile([P, TILES, 2, P], F32, name="straight", bufs=3)
             words = raw[name, n][:].bitcast(F32)[:, :, 256 * g : 256 * (g + 1)]
             nc.vector.tensor_copy(out=tile[:], in_=words.rearrange("m t (w u) -> m t u w", u=2))
-            flat[name, n, g] = tile
+            straight[name, n, g] = tile
 
-        def turn(name, n, g, b, engine):
-            if (name, n, g) not in grouped:
-                grouped[name, n, g] = work.tile([P, GROUP, 2], F32, name="grouped", align_bytes=64, bufs=4)
-            bank = psum.tile([P, 2, 2, P], F32, name="bank_t", bufs=NT)
+        def turn_bank(name, n, g, b, engine):
+            if (name, n, g) not in turned:
+                turned[name, n, g] = work.tile([P, GROUP, 2], F32, name="turned", align_bytes=64, bufs=4)
+            bank = psum.tile([P, 2, 2, P], F32, name="bank_turn", bufs=3)
             for i in range(2):
-                words = raw[name, n][:, 2 * b + i, :].bitcast(F32)
                 for u in range(2):
-                    if (name, n, g) in flat:
-                        block = flat[name, n, g][:, 2 * b + i, u, :]
+                    if (name, n, g) in straight:
+                        block = straight[name, n, g][:, 2 * b + i, u, :]
                     else:
+                        words = raw[name, n][:, 2 * b + i, :].bitcast(F32)
                         block = words[:, 256 * g + u : 256 * (g + 1) : 2]
-                    nc.tensor.transpose(bank[:, i, u, :], block, ident[:])
-            dst = grouped[name, n, g][:, 256 * b : 256 * (b + 1), :].rearrange("p (i r) u -> p i r u", i=2)
-            drain(engine, dst, bank[:].rearrange("p i u r -> p i r u"))
+                    nc.tensor.transpose(bank[:, i, u, :], block, identity[:])
+            tokens = turned[name, n, g][:, HALF * b : HALF * (b + 1), :]
+            move(engine, tokens.rearrange("p (i m) u -> p i m u", i=2), bank[:].rearrange("p i u m -> p i m u"))
+
+        def turn(name, n, g, engines="SS"):
+            for b in range(2):
+                turn_bank(name, n, g, b, engines[b])
 
         def quantize(name, n, g):
-            c = work.tile([P, GROUP], U32, name="codes_" + name, align_bytes=64, bufs=6)
-            s = work.tile([P, GROUP], U8, name="scales_" + name, align_bytes=64, bufs=6)
+            codes[name, n, g] = work.tile([P, GROUP], U32, name="codes_" + name, align_bytes=64, bufs=6)
+            scales[name, n, g] = work.tile([P, GROUP], U8, name="scales_" + name, align_bytes=64, bufs=6)
             nc.vector.quantize_mx(
-                out=c[:].bitcast(FP8X4), scales=s[:], in_=grouped[name, n, g][:].rearrange("p r u -> p (r u)").bitcast(BF16)
+                out=codes[name, n, g][:].bitcast(FP8X4),
+                scales=scales[name, n, g][:],
+                in_=turned[name, n, g][:].rearrange("p m u -> p (m u)").bitcast(BF16),
             )
-            codes[name, n, g] = c
-            scales[name, n, g] = s
 
-        hid = {}
+        relus, mixed = {}, {}
 
-        def stage1(n, hh, js, engines):
-            if (n, hh) not in hid:
-                hid[n, hh] = work.tile([P, T, GROUP], BF16, name="hid", align_bytes=64, bufs=3)
-            planes = hid[n, hh]
-            for j in js:
-                bank = psum.tile([P, GROUP], F32, name="bank_h", bufs=NH)
-                for g in range(2):
-                    cols = slice(P * j, P * (j + 1))
-                    scols = slice(GROUP * hh + P * j, GROUP * hh + P * (j + 1))
-                    nc.tensor.matmul_mx(
-                        out=bank[:],
-                        lhsT=w1_c[hh][:, g, cols].bitcast(FP8X4),
-                        lhsT_scale=w1_s[4 * g : P, scols],
-                        rhs=codes["p", n, g][:].bitcast(FP8X4),
-                        rhs_scale=scales["p", n, g][:],
-                        start=(g == 0),
-                        stop=(g == 1),
-                    )
-                bias = b1_f[:, hh, j : j + 1]
-                if engines[j] == "S":
-                    nc.scalar.activation(out=planes[:, j, :], in_=bank[:], func=ACT.Relu, bias=bias)
-                else:
-                    nc.vector.tensor_scalar(
-                        out=planes[:, j, :], in0=bank[:], scalar1=bias, scalar2=0.0, op0=ALU.add, op1=ALU.max
-                    )
+        def hidden_sums(out, n, h, j, tokens):
+            cols = slice(P * j, P * (j + 1))
+            scale_cols = slice(GROUP * h + P * j, GROUP * h + P * (j + 1))
+            for g in range(PASSES):
+                nc.tensor.matmul_mx(
+                    out=out,
+                    lhsT=w1_codes[h][:, g, cols].bitcast(FP8X4),
+                    lhsT_scale=w1_scale[SCALE_ROWS * g : P, scale_cols],
+                    rhs=codes["p", n, g][:, tokens].bitcast(FP8X4),
+                    rhs_scale=scales["p", n, g][:, tokens],
+                    start=(g == 0),
+                    stop=(g == PASSES - 1),
+                )
 
-        def stage1_half(n, hh, half, pairs, engines):
-            if (n, hh) not in hid:
-                hid[n, hh] = work.tile([P, T, GROUP], BF16, name="hid", align_bytes=64, bufs=3)
-            rows = slice(HALF * half, HALF * (half + 1))
-            for pair in pairs:
-                bank = psum.tile([P, 2, HALF], F32, name="bank_h", bufs=NH)
-                for i in range(2):
-                    j = 2 * pair + i
-                    for g in range(2):
-                        cols = slice(P * j, P * (j + 1))
-                        scols = slice(GROUP * hh + P * j, GROUP * hh + P * (j + 1))
-                        nc.tensor.matmul_mx(
-                            out=bank[:, i, :],
-                            lhsT=w1_c[hh][:, g, cols].bitcast(FP8X4),
-                            lhsT_scale=w1_s[4 * g : P, scols],
-                            rhs=codes["p", n, g][:, rows].bitcast(FP8X4),
-                            rhs_scale=scales["p", n, g][:, rows],
-                            start=(g == 0),
-                            stop=(g == 1),
-                        )
-                for i in range(2):
-                    j = 2 * pair + i
-                    bias = b1_f[:, hh, j : j + 1]
-                    out = hid[n, hh][:, j, rows]
-                    if engines[pair] == "S":
-                        nc.scalar.activation(out=out, in_=bank[:, i, :], func=ACT.Relu, bias=bias)
-                    else:
-                        nc.vector.tensor_scalar(
-                            out=out, in0=bank[:, i, :], scalar1=bias, scalar2=0.0, op0=ALU.add, op1=ALU.max
-                        )
+        def bias_relu(engine, out, in_, h, j):
+            bias = b1_f32[:, h, j : j + 1]
+            if engine == "S":
+                nc.scalar.activation(out=out, in_=in_, func=ACT.Relu, bias=bias)
+            else:
+                nc.vector.tensor_scalar(out=out, in0=in_, scalar1=bias, scalar2=0.0, op0=ALU.add, op1=ALU.max)
 
-        inter = {}
+        def relu_tile(n, h):
+            if (n, h) not in relus:
+                relus[n, h] = work.tile([P, PACK, GROUP], BF16, name="relu", align_bytes=64, bufs=3)
+            return relus[n, h]
 
-        def interleave(n, hh, lo=0, hi=GROUP, cut=None):
-            if (n, hh) not in inter:
-                inter[n, hh] = work.tile([P, GROUP, T], BF16, name="inter", align_bytes=64, bufs=3)
-            q = inter[n, hh]
+        def hidden(n, h, slices, engines="SS"):
+            out = relu_tile(n, h)
+            for j, engine in zip(slices, engines):
+                bank = psum.tile([P, GROUP], F32, name="bank_hidden", bufs=3)
+                hidden_sums(bank[:], n, h, j, slice(0, GROUP))
+                bias_relu(engine, out[:, j, :], bank[:], h, j)
+
+        def hidden_half(n, h, half):
+            out = relu_tile(n, h)
+            tokens = slice(HALF * half, HALF * (half + 1))
+            bank = psum.tile([P, 2, HALF], F32, name="bank_hidden", bufs=3)
+            for j in (2, 3):
+                hidden_sums(bank[:, j - 2, :], n, h, j, tokens)
+            for j in (2, 3):
+                bias_relu("S", out[:, j, tokens], bank[:, j - 2, :], h, j)
+
+        def interleave(n, h, lo=0, hi=GROUP, cut=None):
+            if (n, h) not in mixed:
+                mixed[n, h] = work.tile([P, GROUP, PACK], BF16, name="mixed", align_bytes=64, bufs=3)
             if cut is None:
                 cut = hi
-            dst = q[:].rearrange("p (c i) t -> p c t i", i=4)
-            src = hid[n, hh][:].rearrange("p t (c i) -> p c t i", i=4)
-            nc.vector.tensor_copy(out=dst[:, lo // 4 : cut // 4], in_=src[:, lo // 4 : cut // 4])
+            dst = mixed[n, h][:].rearrange("p (c i) j -> p c j i", i=4)
+            src = relus[n, h][:].rearrange("p j (c i) -> p c j i", i=4)
+            move("V", dst[:, lo // 4 : cut // 4], src[:, lo // 4 : cut // 4])
             if cut < hi:
-                nc.scalar.copy(out=dst[:, cut // 4 : hi // 4], in_=src[:, cut // 4 : hi // 4])
+                move("S", dst[:, cut // 4 : hi // 4], src[:, cut // 4 : hi // 4])
 
-        def quantize_hidden(n, hh, lo=0, hi=GROUP):
-            if ("q", n, hh) not in codes:
-                codes["q", n, hh] = work.tile([P, GROUP], U32, name="codes_q", align_bytes=64, bufs=4)
-                scales["q", n, hh] = work.tile([P, GROUP], U8, name="scales_q", align_bytes=64, bufs=4)
-            c = codes["q", n, hh]
-            s = scales["q", n, hh]
+        def quantize_hidden(n, h, lo=0, hi=GROUP):
+            if ("q", n, h) not in codes:
+                codes["q", n, h] = work.tile([P, GROUP], U32, name="codes_q", align_bytes=64, bufs=4)
+                scales["q", n, h] = work.tile([P, GROUP], U8, name="scales_q", align_bytes=64, bufs=4)
             nc.vector.quantize_mx(
-                out=c[:, lo:hi].bitcast(FP8X4),
-                scales=s[:, lo:hi],
-                in_=inter[n, hh][:, lo:hi, :].rearrange("p r t -> p (r t)"),
+                out=codes["q", n, h][:, lo:hi].bitcast(FP8X4),
+                scales=scales["q", n, h][:, lo:hi],
+                in_=mixed[n, h][:, lo:hi, :].rearrange("p m j -> p (m j)"),
             )
 
         banks = {}
 
-        def product(kind, name, n, weights, k0, tag=None, tiles=(0, T)):
-            if tag is None:
-                tag, nb = "bank_" + kind, 1
-            else:
-                nb = NH
-            bank = psum.tile([P, T, K], F32, name=tag, bufs=nb)
+        def token_product(kind, n, name, weight_codes, first_row, bank, tiles):
             for t in range(*tiles):
                 banks[kind, n, t] = bank
                 cols = slice(P * t, P * (t + 1))
-                for g in range(2):
+                for g in range(PASSES):
                     nc.tensor.matmul_mx(
                         out=bank[:, t, :],
                         lhsT=codes[name, n, g][:, cols].bitcast(FP8X4),
                         lhsT_scale=scales[name, n, g][:, cols],
-                        rhs=weights[:, g, :].bitcast(FP8X4),
-                        rhs_scale=small_s[k0 + 4 * g : P, :],
+                        rhs=weight_codes[:, g, :].bitcast(FP8X4),
+                        rhs_scale=small_scales[first_row + SCALE_ROWS * g : P, :],
                         start=(g == 0),
-                        stop=(g == 1),
+                        stop=(g == PASSES - 1),
                     )
 
-        rd, neg_max, gate, total, inv, result, result_bf = {}, {}, {}, {}, {}, {}, {}
+        def rewards(n):
+            bank = psum.tile([P, TILES, K], F32, name="bank_rewards")
+            token_product("r", n, "x", wr_codes, wr_row, bank, (0, TILES))
+
+        def logits(n):
+            bank = psum.tile([P, TILES, K], F32, name="bank_logits")
+            token_product("logits", n, "q", w2_codes, w2_row, bank, (0, TILES))
+
+        def logits_half(n, half):
+            bank = psum.tile([P, TILES, K], F32, name="bank_hidden", bufs=3)
+            token_product("logits", n, "q", w2_codes, w2_row, bank, (2 * half, 2 * half + 2))
+
+        neg_lam = keep.tile([P, K], F32, name="neg_lam")
+        neg_max, gate, total, debiased, result, result_bf16, plane_scales = {}, {}, {}, {}, {}, {}, {}
+
+        def spread_lam():
+            bank = psum.tile([P, TILES, K], F32, name="bank_rewards")
+            nc.tensor.matmul(bank[:, 0, :], lhsT=ones[:], rhs=lam_row[:], start=True, stop=True)
+            nc.vector.tensor_scalar(out=neg_lam[:], in0=bank[:, 0, :], scalar1=-1.0, scalar2=None, op0=ALU.mult)
 
         def debias(n):
-            rd[n] = work.tile([P, T, K], F32, name="rd", bufs=2)
-            for t in range(T):
-                r = banks["r", n, t]
+            debiased[n] = work.tile([P, TILES, K], F32, name="debiased")
+            for t in range(TILES):
+                r = banks["r", n, t][:, t, :]
                 nc.vector.scalar_tensor_tensor(
-                    out=rd[n][:, t, :], in0=neg_lam[:], scalar=r[:, t, 0:1], in1=r[:, t, :], op0=ALU.mult, op1=ALU.add
+                    out=debiased[n][:, t, :], in0=neg_lam[:], scalar=r[:, 0:1], in1=r, op0=ALU.mult, op1=ALU.add
                 )
 
-        def row_max(n, lo=0, hi=T):
-            tiles = (lo, hi)
+        def row_max(n, lo=0, hi=TILES):
             if n not in neg_max:
-                neg_max[n] = work.tile([P, T], F32, name="neg_max", bufs=2)
-            ts = slice(*tiles)
+                neg_max[n] = work.tile([P, TILES], F32, name="neg_max")
+            bank = banks["logits", n, lo]
             nc.vector.tensor_reduce(
-                out=neg_max[n][:, ts], in_=banks["l", n, tiles[0]][:, ts, :], axis=AX.X, op=ALU.max, negate=True
+                out=neg_max[n][:, lo:hi], in_=bank[:, lo:hi, :], axis=AX.X, op=ALU.max, negate=True
             )
 
-        def exps(n, lo=0, hi=T):
-            tiles = (lo, hi)
+        def exps(n, lo=0, hi=TILES):
             if n not in gate:
-                gate[n] = work.tile([P, T, K], F32, name="gate", bufs=2)
-                total[n] = work.tile([P, T], F32, name="total", bufs=2)
-            for t in range(*tiles):
+                gate[n] = work.tile([P, TILES, K], F32, name="gate")
+                total[n] = work.tile([P, TILES], F32, name="total")
+            for t in range(lo, hi):
                 nc.scalar.activation(
                     out=gate[n][:, t, :],
-                    in_=banks["l", n, t][:, t, :],
+                    in_=banks["logits", n, t][:, t, :],
                     func=ACT.Exp,
                     bias=neg_max[n][:, t : t + 1],
                     accum_out=total[n][:, t : t + 1],
                 )
 
-        def combine(n, tiles=(0, T)):
-            scaled = work.tile([P, T], F32, name="scaled", bufs=2)
-            inv[n] = work.tile([P, T], F32, name="inv", bufs=2)
-            ts = slice(*tiles)
-            nc.vector.tensor_scalar(out=scaled[:, ts], in0=total[n][:, ts], scalar1=1.0 / K, scalar2=None, op0=ALU.mult)
-            nc.vector.reciprocal(out=inv[n][:, ts], in_=scaled[:, ts])
-            if n not in result:
-                result[n] = work.tile([P, T, K], F32, name="result", bufs=2)
-            for t in range(*tiles):
+        def combine(n):
+            mean = work.tile([P, TILES], F32, name="mean")
+            inverse = work.tile([P, TILES], F32, name="inverse")
+            nc.vector.tensor_scalar(out=mean[:], in0=total[n][:], scalar1=1.0 / K, scalar2=None, op0=ALU.mult)
+            nc.vector.reciprocal(out=inverse[:], in_=mean[:])
+            result[n] = work.tile([P, TILES, K], F32, name="result")
+            for t in range(TILES):
                 nc.vector.scalar_tensor_tensor(
                     out=result[n][:, t, :],
                     in0=gate[n][:, t, :],
-                    scalar=inv[n][:, t : t + 1],
-                    in1=rd[n][:, t, :],
+                    scalar=inverse[:, t : t + 1],
+                    in1=debiased[n][:, t, :],
                     op0=ALU.mult,
                     op1=ALU.mult,
                 )
-            rows = out_0[GROUP * n : GROUP * (n + 1), :].rearrange("(m t) k -> m t k", t=T)
-            nc.sync.dma_start(out=rows[:, ts, :], in_=result[n][:, ts, :])
+            rows = out_0[GROUP * n : GROUP * (n + 1), :].rearrange("(m t) k -> m t k", t=TILES)
+            nc.sync.dma_start(out=rows, in_=result[n][:])
 
         def cast(n, engine="V"):
-            result_bf[n] = work.tile([P, K, T], BF16, name="result_bf", align_bytes=64, bufs=2)
-            drain(engine, result_bf[n][:], result[n][:].rearrange("p t k -> p k t"))
+            result_bf16[n] = work.tile([P, K, TILES], BF16, name="result_bf16", align_bytes=64)
+            move(engine, result_bf16[n][:], result[n][:].rearrange("m t k -> m k t"))
 
-        out_scales = {}
-
-        def planes_out(n):
-            c = work.tile([P, K], U32, name="out_c", align_bytes=64, bufs=2)
-            if n % 2 == 0:
-                out_scales[n // 2] = work.tile([P, K], U8, name="out_s", align_bytes=64, bufs=2)
-            s = out_scales[n // 2]
+        def store_planes(n):
+            words = work.tile([P, K], U32, name="out_words", align_bytes=64)
+            odd = n % 2
+            if not odd:
+                plane_scales[n // 2] = work.tile([P, K], U8, name="out_scales", align_bytes=64)
+            pair = plane_scales[n // 2]
             nc.vector.quantize_mx(
-                out=c[:].bitcast(FP8X4),
-                scales=s[4 * (n % 2) : P, :],
-                in_=result_bf[n][:].rearrange("p k t -> p (k t)"),
+                out=words[:].bitcast(FP8X4),
+                scales=pair[SCALE_ROWS * odd : P, :],
+                in_=result_bf16[n][:].rearrange("m k t -> m (k t)"),
             )
-            nc.sync.dma_start(out=out_1[n].rearrange("p k t -> p (k t)").bitcast(I32), in_=c[:].bitcast(I32))
-            if n % 2 == 1:
-                for Q in range(4):
+            nc.sync.dma_start(out=out_1[n].rearrange("m k t -> m (k t)").bitcast(I32), in_=words[:].bitcast(I32))
+            if odd:
+                for quadrant in range(4):
                     nc.sync.dma_start(
-                        out=out_2[n - 1 : n + 1, 4 * Q : 4 * Q + 4, :].bitcast(I32),
-                        in_=s[32 * Q : 32 * Q + 8, :].bitcast(I32),
+                        out=out_2[n - 1 : n + 1, SCALE_ROWS * quadrant : SCALE_ROWS * (quadrant + 1), :].bitcast(I32),
+                        in_=pair[32 * quadrant : 32 * quadrant + 2 * SCALE_ROWS, :].bitcast(I32),
                     )
 
-        def turns(name, n, g, engines="SS"):
-            for b in range(2):
-                turn(name, n, g, b, engines[b])
-
-        def warm_up(count):
-            for i in range(count):
-                bank = psum.tile([P, 512], F32, name="bank_l", bufs=1)
-                nc.tensor.matmul(bank[:], lhsT=ones[:], rhs=zeros[:], start=True, stop=True)
-
-        turn("p", 0, 0, 0, "S")
-        turn("p", 0, 1, 0, "S")
-        permute_w1(0)
-        permute_w1_scales(0)
-        turn("p", 0, 0, 1, "S")
-        turn("p", 0, 1, 1, "S")
-        warm_up(WARM[0])
+        turn_bank("p", 0, 0, 0, "S")
+        turn_bank("p", 0, 1, 0, "S")
+        reorder_w1(0)
+        reorder_w1_scales(0)
+        turn_bank("p", 0, 0, 1, "S")
+        turn_bank("p", 0, 1, 1, "S")
         quantize("p", 0, 0)
         quantize("p", 0, 1)
-        b1_f = keep.tile([P, 2, T], F32, name="b1_f")
-        nc.vector.tensor_copy(out=b1_f[:], in_=b1_bf[:])
-        permute_w1_scales(1)
-        permute_w1(1)
+        b1_f32 = keep.tile([P, 2, PACK], F32, name="b1_f32")
+        nc.vector.tensor_copy(out=b1_f32[:], in_=b1_columns[:])
+        reorder_w1_scales(1)
+        reorder_w1(1)
 
-        def lam_prep():
-            lam_bank = psum.tile([P, T, K], F32, name="bank_r", bufs=1)
-            nc.tensor.matmul(lam_bank[:, 0, :], lhsT=ones[:], rhs=lam_row[:], start=True, stop=True)
-            nc.vector.tensor_scalar(out=neg_lam[:], in0=lam_bank[:, 0, :], scalar1=-1.0, scalar2=None, op0=ALU.mult)
-
-        neg_lam = keep.tile([P, K], F32, name="neg_lam")
-        steps = {
-            "T": lambda name, n, g: turns(name, n, g, ENG.get(("T", name, n, g), "SS")),
-            "A": lambda n, hh, pair: stage1(n, hh, (2 * pair, 2 * pair + 1), ENG.get(("A", n, hh, pair), "SS") * 2),
-            "Ah": lambda n, hh, half: stage1_half(n, hh, half, (1,), "SS"),
-            "Q": quantize,
-            "st": straighten,
-            "I": interleave,
-            "QQ": quantize_hidden,
-            "RR": lambda n: product("r", "x", n, wr_c, 0),
-            "S2": lambda n: product("l", "q", n, w2_c, 8),
-            "S2h": lambda n, lo, hi: product("l", "q", n, w2_c, 8, "bank_h", (lo, hi)),
-            "max": row_max,
-            "exp": exps,
-            "rd": debias,
-            "comb": combine,
-            "cast": cast,
-            "out": planes_out,
-            "lam": lam_prep,
-        }
-        for step in PROGRAM:
-            steps[step[0]](*step[1:])
+        straighten("p", 1, 0)
+        hidden(0, 0, (2, 3))
+        straighten("p", 1, 1)
+        hidden(0, 0, (0, 1))
+        straighten("x", 0, 0)
+        turn("p", 1, 0, "VS")
+        interleave(0, 0)
+        quantize("p", 1, 0)
+        hidden(0, 1, (2, 3), "SV")
+        turn("p", 1, 1)
+        spread_lam()
+        hidden(0, 1, (0, 1))
+        turn("x", 0, 0)
+        quantize("p", 1, 1)
+        straighten("x", 0, 1)
+        interleave(0, 1, 0, GROUP, 448)
+        straighten("p", 2, 0)
+        hidden(1, 0, (2, 3), "SV")
+        turn("p", 2, 1)
+        hidden(1, 1, (0, 1))
+        turn("x", 0, 1)
+        quantize_hidden(0, 1)
+        quantize("x", 0, 0)
+        straighten("x", 1, 0)
+        quantize_hidden(0, 0)
+        quantize("p", 2, 1)
+        hidden(1, 0, (0, 1))
+        quantize("x", 0, 1)
+        turn("p", 2, 0, "SV")
+        hidden(1, 1, (2, 3))
+        turn("x", 1, 0)
+        straighten("x", 2, 0)
+        quantize("p", 2, 0)
+        logits(0)
+        interleave(1, 0)
+        row_max(0)
+        turn("p", 3, 0)
+        hidden(2, 0, (2, 3))
+        interleave(1, 1)
+        turn("x", 1, 1)
+        quantize_hidden(1, 0)
+        hidden(2, 0, (0, 1))
+        quantize_hidden(1, 1)
+        quantize("p", 3, 0)
+        exps(0)
+        quantize("x", 1, 0)
+        quantize("x", 1, 1)
+        rewards(0)
+        hidden(2, 1, (2, 3))
+        turn("p", 3, 1)
+        hidden(2, 1, (0, 1))
+        logits(1)
+        debias(0)
+        interleave(2, 0)
+        combine(0)
+        quantize_hidden(2, 0)
+        quantize("p", 3, 1)
+        row_max(1)
+        interleave(2, 1)
+        turn("x", 2, 0)
+        exps(1)
+        quantize("x", 2, 0)
+        rewards(1)
+        quantize_hidden(2, 1)
+        hidden(3, 0, (0, 1))
+        cast(0)
+        turn("x", 2, 1)
+        debias(1)
+        hidden(3, 0, (2, 3))
+        combine(1)
+        quantize("x", 2, 1)
+        logits(2)
+        cast(1)
+        hidden_half(3, 1, 0)
+        row_max(2)
+        store_planes(0)
+        turn("x", 3, 0)
+        rewards(2)
+        interleave(3, 0)
+        exps(2)
+        quantize("x", 3, 0)
+        turn("x", 3, 1)
+        hidden(3, 1, (0, 1))
+        store_planes(1)
+        debias(2)
+        quantize_hidden(3, 0)
+        quantize("x", 3, 1)
+        hidden_half(3, 1, 1)
+        combine(2)
+        interleave(3, 1, 0, HALF, 160)
+        interleave(3, 1, HALF, GROUP, 416)
+        quantize_hidden(3, 1, 0, HALF)
+        quantize_hidden(3, 1, HALF, GROUP)
+        rewards(3)
+        logits_half(3, 0)
+        row_max(3, 0, 2)
+        cast(2, "S")
+        exps(3, 0, 2)
+        logits_half(3, 1)
+        row_max(3, 2, 4)
+        store_planes(2)
+        exps(3, 2, 4)
+        debias(3)
+        combine(3)
+        cast(3)
+        store_planes(3)

from contextlib import ExitStack

import concourse.mybir as mybir
from concourse.masks import make_identity

N, D, H, K = 2048, 1024, 1024, 128
FLOPS = 2 * N * D * H + 2 * N * D * K + 2 * N * H * K

F32 = mybir.dt.float32
BF16 = mybir.dt.bfloat16
I32 = mybir.dt.int32
U32 = mybir.dt.uint32
U8 = mybir.dt.uint8
FP8X4 = mybir.dt.float8_e4m3fn_x4
ACT = mybir.ActivationFunctionType
ALU = mybir.AluOpType
AX = mybir.AxisListType

P = 128
PACK = 4
GROUP = P * PACK
HALF = GROUP // 2
GROUPS = N // GROUP
PASSES = 2
TILES = GROUP // P
SCALE_ROWS = 4


def tile_armoverbositydebiasedgatedobjectives_x2_kernel(
    tc, x, p, wr_words, wr_scales, w1_words, w1_scales, b1, w2_words, w2_scales, lam, out_0, out_1, out_2
):
    nc = tc.nc
    with ExitStack() as ctx:
        keep = ctx.enter_context(tc.tile_pool(name="keep", bufs=1))
        work = ctx.enter_context(tc.tile_pool(name="work", bufs=2))
        psum = ctx.enter_context(tc.psum_pool(name="psum", bufs=1))
        ctx.enter_context(tc.manual_schedule())

        w1_raw_scales = keep.tile([P, H], U8, name="w1_raw_scales", align_bytes=64)
        nc.vector.memset(w1_raw_scales[:].bitcast(I32), 0)
        small_scales = keep.tile([P, K], U8, name="small_scales", align_bytes=64)
        nc.vector.memset(small_scales[:].bitcast(I32), 0)
        wr_row, w2_row = 0, PASSES * SCALE_ROWS

        zero = keep.tile([P, P], BF16, name="zero")
        nc.vector.memset(zero[:], 0.0)
        identity = keep.tile([P, P], F32, name="identity")
        make_identity(nc, identity[:])
        lam_row = keep.tile([P, K], BF16, name="lam_row")
        nc.vector.memset(lam_row[:], 0.0)

        def load_scales(queue, tile, scales, first_row):
            for quadrant in range(4):
                first = 32 * quadrant + first_row
                queue.dma_start(
                    out=tile[first : first + PASSES * SCALE_ROWS, :].bitcast(I32),
                    in_=scales[:, SCALE_ROWS * quadrant : SCALE_ROWS * (quadrant + 1), :].bitcast(I32),
                )

        raw = {}

        def load(name, source, n, lo=0, hi=TILES):
            if (name, n) not in raw:
                raw[name, n] = keep.tile([P, TILES, D], BF16, name="raw_%s%d" % (name, n), align_bytes=64)
            rows = source[GROUP * n : GROUP * (n + 1), :].rearrange("(m t) k -> m t k", t=TILES)
            nc.sync.dma_start(out=raw[name, n][:, lo:hi, :], in_=rows[:, lo:hi, :])

        def load_words(source, name, lo, hi):
            tile = keep.tile([P, PASSES, hi - lo], U32, name=name, align_bytes=64)
            words = source.rearrange("g p n t -> g p (n t)")[:, :, PACK * lo : PACK * hi].bitcast(I32)
            nc.sync.dma_start(out=tile[:].bitcast(I32), in_=words.rearrange("g p n -> p g n"))
            return tile

        load_scales(nc.scalar, w1_raw_scales, w1_scales, 0)
        ones = keep.tile([P, P], BF16, name="ones")
        nc.scalar.activation(out=ones[:], in_=zero[:], func=ACT.Exp)
        load("p", p, 0, 0, 2)
        load("p", p, 0, 2, TILES)
        w1_raw = [load_words(w1_words, "w1_raw0", 0, GROUP)]
        w1_raw.append(load_words(w1_words, "w1_raw1", GROUP, H))
        nc.gpsimd.dma_start(out=lam_row[0:1, :], in_=lam.rearrange("(o k) -> o k", o=1))
        b1_columns = keep.tile([P, 2, PACK], BF16, name="b1_columns")
        nc.gpsimd.dma_start(out=b1_columns[:], in_=b1.rearrange("(h m j) -> m h j", h=2, j=PACK))
        load("p", p, 1)
        load("x", x, 0)
        wr_codes = load_words(wr_words, "wr_codes", 0, K)
        w2_codes = load_words(w2_words, "w2_codes", 0, K)
        load_scales(nc.sync, small_scales, wr_scales, wr_row)
        load_scales(nc.sync, small_scales, w2_scales, w2_row)
        load("p", p, 2)
        load("x", x, 1)
        load("p", p, 3)
        load("x", x, 2)
        load("x", x, 3)

        w1_codes = []
        w1_scale = keep.tile([P, H], U8, name="w1_scale", align_bytes=64)

        def reorder_w1(h):
            tile = keep.tile([P, PASSES, GROUP], U32, name="w1_codes%d" % h, align_bytes=64)
            for g in range(PASSES):
                nc.vector.tensor_copy(
                    out=tile[:, g, :].bitcast(I32).rearrange("p (j m) -> p j m", j=PACK),
                    in_=w1_raw[h][:, g, :].bitcast(I32).rearrange("p (m j) -> p j m", j=PACK),
                )
            w1_codes.append(tile)

        def reorder_w1_scales(h):
            cols = slice(GROUP * h, GROUP * (h + 1))
            nc.vector.tensor_copy(
                out=w1_scale[:, cols].rearrange("p (j m) -> p j m", j=PACK),
                in_=w1_raw_scales[:, cols].rearrange("p (m j) -> p j m", j=PACK),
            )

        turned, straight, codes, scales = {}, {}, {}, {}

        def move(engine, out, in_):
            if engine == "S":
                nc.scalar.copy(out=out, in_=in_)
            else:
                nc.vector.tensor_copy(out=out, in_=in_)

        def straighten(name, n, g):
            tile = work.tile([P, TILES, 2, P], F32, name="straight", bufs=3)
            words = raw[name, n][:].bitcast(F32)[:, :, 256 * g : 256 * (g + 1)]
            nc.vector.tensor_copy(out=tile[:], in_=words.rearrange("m t (w u) -> m t u w", u=2))
            straight[name, n, g] = tile

        def turn_bank(name, n, g, b, engine):
            if (name, n, g) not in turned:
                turned[name, n, g] = work.tile([P, GROUP, 2], F32, name="turned", align_bytes=64, bufs=4)
            bank = psum.tile([P, 2, 2, P], F32, name="bank_turn", bufs=3)
            for i in range(2):
                for u in range(2):
                    if (name, n, g) in straight:
                        block = straight[name, n, g][:, 2 * b + i, u, :]
                    else:
                        words = raw[name, n][:, 2 * b + i, :].bitcast(F32)
                        block = words[:, 256 * g + u : 256 * (g + 1) : 2]
                    nc.tensor.transpose(bank[:, i, u, :], block, identity[:])
            tokens = turned[name, n, g][:, HALF * b : HALF * (b + 1), :]
            move(engine, tokens.rearrange("p (i m) u -> p i m u", i=2), bank[:].rearrange("p i u m -> p i m u"))

        def turn(name, n, g, engines="SS"):
            for b in range(2):
                turn_bank(name, n, g, b, engines[b])

        def quantize(name, n, g):
            codes[name, n, g] = work.tile([P, GROUP], U32, name="codes_" + name, align_bytes=64, bufs=6)
            scales[name, n, g] = work.tile([P, GROUP], U8, name="scales_" + name, align_bytes=64, bufs=6)
            nc.vector.quantize_mx(
                out=codes[name, n, g][:].bitcast(FP8X4),
                scales=scales[name, n, g][:],
                in_=turned[name, n, g][:].rearrange("p m u -> p (m u)").bitcast(BF16),
            )

        relus, mixed = {}, {}

        def hidden_sums(out, n, h, j, tokens):
            cols = slice(P * j, P * (j + 1))
            scale_cols = slice(GROUP * h + P * j, GROUP * h + P * (j + 1))
            for g in range(PASSES):
                nc.tensor.matmul_mx(
                    out=out,
                    lhsT=w1_codes[h][:, g, cols].bitcast(FP8X4),
                    lhsT_scale=w1_scale[SCALE_ROWS * g : P, scale_cols],
                    rhs=codes["p", n, g][:, tokens].bitcast(FP8X4),
                    rhs_scale=scales["p", n, g][:, tokens],
                    start=(g == 0),
                    stop=(g == PASSES - 1),
                )

        def bias_relu(engine, out, in_, h, j):
            bias = b1_f32[:, h, j : j + 1]
            if engine == "S":
                nc.scalar.activation(out=out, in_=in_, func=ACT.Relu, bias=bias)
            else:
                nc.vector.tensor_scalar(out=out, in0=in_, scalar1=bias, scalar2=0.0, op0=ALU.add, op1=ALU.max)

        def relu_tile(n, h):
            if (n, h) not in relus:
                relus[n, h] = work.tile([P, PACK, GROUP], BF16, name="relu", align_bytes=64, bufs=3)
            return relus[n, h]

        def hidden(n, h, slices, engines="SS"):
            out = relu_tile(n, h)
            for j, engine in zip(slices, engines):
                bank = psum.tile([P, GROUP], F32, name="bank_hidden", bufs=3)
                hidden_sums(bank[:], n, h, j, slice(0, GROUP))
                bias_relu(engine, out[:, j, :], bank[:], h, j)

        def hidden_half(n, h, half):
            out = relu_tile(n, h)
            tokens = slice(HALF * half, HALF * (half + 1))
            bank = psum.tile([P, 2, HALF], F32, name="bank_hidden", bufs=3)
            for j in (2, 3):
                hidden_sums(bank[:, j - 2, :], n, h, j, tokens)
            for j in (2, 3):
                bias_relu("S", out[:, j, tokens], bank[:, j - 2, :], h, j)

        def interleave(n, h, lo=0, hi=GROUP, cut=None):
            if (n, h) not in mixed:
                mixed[n, h] = work.tile([P, GROUP, PACK], BF16, name="mixed", align_bytes=64, bufs=3)
            if cut is None:
                cut = hi
            dst = mixed[n, h][:].rearrange("p (c i) j -> p c j i", i=4)
            src = relus[n, h][:].rearrange("p j (c i) -> p c j i", i=4)
            move("V", dst[:, lo // 4 : cut // 4], src[:, lo // 4 : cut // 4])
            if cut < hi:
                move("S", dst[:, cut // 4 : hi // 4], src[:, cut // 4 : hi // 4])

        def quantize_hidden(n, h, lo=0, hi=GROUP):
            if ("q", n, h) not in codes:
                codes["q", n, h] = work.tile([P, GROUP], U32, name="codes_q", align_bytes=64, bufs=4)
                scales["q", n, h] = work.tile([P, GROUP], U8, name="scales_q", align_bytes=64, bufs=4)
            nc.vector.quantize_mx(
                out=codes["q", n, h][:, lo:hi].bitcast(FP8X4),
                scales=scales["q", n, h][:, lo:hi],
                in_=mixed[n, h][:, lo:hi, :].rearrange("p m j -> p (m j)"),
            )

        banks = {}

        def token_product(kind, n, name, weight_codes, first_row, bank, tiles):
            for t in range(*tiles):
                banks[kind, n, t] = bank
                cols = slice(P * t, P * (t + 1))
                for g in range(PASSES):
                    nc.tensor.matmul_mx(
                        out=bank[:, t, :],
                        lhsT=codes[name, n, g][:, cols].bitcast(FP8X4),
                        lhsT_scale=scales[name, n, g][:, cols],
                        rhs=weight_codes[:, g, :].bitcast(FP8X4),
                        rhs_scale=small_scales[first_row + SCALE_ROWS * g : P, :],
                        start=(g == 0),
                        stop=(g == PASSES - 1),
                    )

        def rewards(n):
            bank = psum.tile([P, TILES, K], F32, name="bank_rewards")
            token_product("r", n, "x", wr_codes, wr_row, bank, (0, TILES))

        def logits(n):
            bank = psum.tile([P, TILES, K], F32, name="bank_logits")
            token_product("logits", n, "q", w2_codes, w2_row, bank, (0, TILES))

        def logits_half(n, half):
            bank = psum.tile([P, TILES, K], F32, name="bank_hidden", bufs=3)
            token_product("logits", n, "q", w2_codes, w2_row, bank, (2 * half, 2 * half + 2))

        neg_lam = keep.tile([P, K], F32, name="neg_lam")
        neg_max, gate, total, debiased, result, result_bf16, plane_scales = {}, {}, {}, {}, {}, {}, {}

        def spread_lam():
            bank = psum.tile([P, TILES, K], F32, name="bank_rewards")
            nc.tensor.matmul(bank[:, 0, :], lhsT=ones[:], rhs=lam_row[:], start=True, stop=True)
            nc.vector.tensor_scalar(out=neg_lam[:], in0=bank[:, 0, :], scalar1=-1.0, scalar2=None, op0=ALU.mult)

        def debias(n):
            debiased[n] = work.tile([P, TILES, K], F32, name="debiased")
            for t in range(TILES):
                r = banks["r", n, t][:, t, :]
                nc.vector.scalar_tensor_tensor(
                    out=debiased[n][:, t, :], in0=neg_lam[:], scalar=r[:, 0:1], in1=r, op0=ALU.mult, op1=ALU.add
                )

        def row_max(n, lo=0, hi=TILES):
            if n not in neg_max:
                neg_max[n] = work.tile([P, TILES], F32, name="neg_max")
            bank = banks["logits", n, lo]
            nc.vector.tensor_reduce(
                out=neg_max[n][:, lo:hi], in_=bank[:, lo:hi, :], axis=AX.X, op=ALU.max, negate=True
            )

        def exps(n, lo=0, hi=TILES):
            if n not in gate:
                gate[n] = work.tile([P, TILES, K], F32, name="gate")
                total[n] = work.tile([P, TILES], F32, name="total")
            for t in range(lo, hi):
                nc.scalar.activation(
                    out=gate[n][:, t, :],
                    in_=banks["logits", n, t][:, t, :],
                    func=ACT.Exp,
                    bias=neg_max[n][:, t : t + 1],
                    accum_out=total[n][:, t : t + 1],
                )

        def combine(n):
            mean = work.tile([P, TILES], F32, name="mean")
            inverse = work.tile([P, TILES], F32, name="inverse")
            nc.vector.tensor_scalar(out=mean[:], in0=total[n][:], scalar1=1.0 / K, scalar2=None, op0=ALU.mult)
            nc.vector.reciprocal(out=inverse[:], in_=mean[:])
            result[n] = work.tile([P, TILES, K], F32, name="result")
            for t in range(TILES):
                nc.vector.scalar_tensor_tensor(
                    out=result[n][:, t, :],
                    in0=gate[n][:, t, :],
                    scalar=inverse[:, t : t + 1],
                    in1=debiased[n][:, t, :],
                    op0=ALU.mult,
                    op1=ALU.mult,
                )
            rows = out_0[GROUP * n : GROUP * (n + 1), :].rearrange("(m t) k -> m t k", t=TILES)
            nc.sync.dma_start(out=rows, in_=result[n][:])

        def cast(n, engine="V"):
            result_bf16[n] = work.tile([P, K, TILES], BF16, name="result_bf16", align_bytes=64)
            move(engine, result_bf16[n][:], result[n][:].rearrange("m t k -> m k t"))

        def store_planes(n):
            words = work.tile([P, K], U32, name="out_words", align_bytes=64)
            odd = n % 2
            if not odd:
                plane_scales[n // 2] = work.tile([P, K], U8, name="out_scales", align_bytes=64)
            pair = plane_scales[n // 2]
            nc.vector.quantize_mx(
                out=words[:].bitcast(FP8X4),
                scales=pair[SCALE_ROWS * odd : P, :],
                in_=result_bf16[n][:].rearrange("m k t -> m (k t)"),
            )
            nc.sync.dma_start(out=out_1[n].rearrange("m k t -> m (k t)").bitcast(I32), in_=words[:].bitcast(I32))
            if odd:
                for quadrant in range(4):
                    nc.sync.dma_start(
                        out=out_2[n - 1 : n + 1, SCALE_ROWS * quadrant : SCALE_ROWS * (quadrant + 1), :].bitcast(I32),
                        in_=pair[32 * quadrant : 32 * quadrant + 2 * SCALE_ROWS, :].bitcast(I32),
                    )

        turn_bank("p", 0, 0, 0, "S")
        turn_bank("p", 0, 1, 0, "S")
        reorder_w1(0)
        reorder_w1_scales(0)
        turn_bank("p", 0, 0, 1, "S")
        turn_bank("p", 0, 1, 1, "S")
        quantize("p", 0, 0)
        quantize("p", 0, 1)
        b1_f32 = keep.tile([P, 2, PACK], F32, name="b1_f32")
        nc.vector.tensor_copy(out=b1_f32[:], in_=b1_columns[:])
        reorder_w1_scales(1)
        reorder_w1(1)

        straighten("p", 1, 0)
        hidden(0, 0, (2, 3))
        straighten("p", 1, 1)
        hidden(0, 0, (0, 1))
        straighten("x", 0, 0)
        turn("p", 1, 0, "VS")
        interleave(0, 0)
        quantize("p", 1, 0)
        hidden(0, 1, (2, 3), "SV")
        turn("p", 1, 1)
        spread_lam()
        hidden(0, 1, (0, 1))
        turn("x", 0, 0)
        quantize("p", 1, 1)
        straighten("x", 0, 1)
        interleave(0, 1, 0, GROUP, 448)
        straighten("p", 2, 0)
        hidden(1, 0, (2, 3), "SV")
        turn("p", 2, 1)
        hidden(1, 1, (0, 1))
        turn("x", 0, 1)
        quantize_hidden(0, 1)
        quantize("x", 0, 0)
        straighten("x", 1, 0)
        quantize_hidden(0, 0)
        quantize("p", 2, 1)
        hidden(1, 0, (0, 1))
        quantize("x", 0, 1)
        turn("p", 2, 0, "SV")
        hidden(1, 1, (2, 3))
        turn("x", 1, 0)
        straighten("x", 2, 0)
        quantize("p", 2, 0)
        logits(0)
        interleave(1, 0)
        row_max(0)
        turn("p", 3, 0)
        hidden(2, 0, (2, 3))
        interleave(1, 1)
        turn("x", 1, 1)
        quantize_hidden(1, 0)
        hidden(2, 0, (0, 1))
        quantize_hidden(1, 1)
        quantize("p", 3, 0)
        exps(0)
        quantize("x", 1, 0)
        quantize("x", 1, 1)
        rewards(0)
        hidden(2, 1, (2, 3))
        turn("p", 3, 1)
        hidden(2, 1, (0, 1))
        logits(1)
        debias(0)
        interleave(2, 0)
        combine(0)
        quantize_hidden(2, 0)
        quantize("p", 3, 1)
        row_max(1)
        interleave(2, 1)
        turn("x", 2, 0)
        exps(1)
        quantize("x", 2, 0)
        rewards(1)
        quantize_hidden(2, 1)
        hidden(3, 0, (0, 1))
        cast(0)
        turn("x", 2, 1)
        debias(1)
        hidden(3, 0, (2, 3))
        combine(1)
        quantize("x", 2, 1)
        logits(2)
        cast(1)
        hidden_half(3, 1, 0)
        row_max(2)
        store_planes(0)
        turn("x", 3, 0)
        rewards(2)
        interleave(3, 0)
        exps(2)
        quantize("x", 3, 0)
        turn("x", 3, 1)
        hidden(3, 1, (0, 1))
        store_planes(1)
        debias(2)
        quantize_hidden(3, 0)
        quantize("x", 3, 1)
        hidden_half(3, 1, 1)
        combine(2)
        interleave(3, 1, 0, HALF, 160)
        interleave(3, 1, HALF, GROUP, 416)
        quantize_hidden(3, 1, 0, HALF)
        quantize_hidden(3, 1, HALF, GROUP)
        rewards(3)
        logits_half(3, 0)
        row_max(3, 0, 2)
        cast(2, "S")
        exps(3, 0, 2)
        logits_half(3, 1)
        row_max(3, 2, 4)
        store_planes(2)
        exps(3, 2, 4)
        debias(3)
        combine(3)
        cast(3)
        store_planes(3)
